import numpy as np, ml_dtypes
CORES = [16,17,18,19,32,33,34,35]
N = 8
import mx_ref
BF = ml_dtypes.bfloat16
def tile(rs):
    return np.stack(rs, axis=2).reshape(128, -1).astype(BF)
def cut(t, i, w=512):
    return t[:, w * i:w * i + w]
def pick(q, e):
    c = np.concatenate([q[0].reshape(128, -1, 4), np.zeros((128, 1, 4), np.uint8)], axis=1); s = np.concatenate([q[1], np.ones((16, 1), np.uint8)], axis=1)
    return (np.ascontiguousarray(c[:, e].reshape(128, -1)), np.ascontiguousarray(s[:, e]))
def join(*qs):
    return (np.concatenate([q[0] for q in qs], axis=1), np.concatenate([q[1] for q in qs], axis=1))
def put(q, e, v):
    c, s = q[0].reshape(128, -1, 4).copy(), q[1].copy(); c[:, e] = v[0].reshape(128, -1, 4); s[:, e] = v[1]
    return (c.reshape(128, -1), s)
def pk(c, s):
    return (np.ascontiguousarray(c), mx_ref.live(s))
def emit(q):
    return q[0], q[1]
def packed(v, rng):
    q = [mx_ref.quantize(np.ascontiguousarray(v[r])) for r in range(N)]
    return np.stack([a for a, b in q]), np.stack([mx_ref.plane(b, rng) for a, b in q])
def values_of_codes():
    e, c = np.zeros((128, 128, 4), np.float32), np.zeros((128, 2, 4), np.uint8)
    e[np.arange(128), np.arange(128), 0] = 1
    c[:127, :, 0] = np.arange(256).reshape(2, 128).T[:127]
    return mx_ref.matmul(mx_ref.quantize(e.reshape(128, 512).astype(BF)), (c.reshape(128, 8), np.full((16, 2), 127, np.uint8))).T.reshape(-1).astype(np.float64)
CODE_VALUE, SCALE_VALUE = values_of_codes(), 2.0 ** (np.arange(256) - 127.0)
def decode(q):
    return (CODE_VALUE[q[0]].reshape(16, 8, -1, 4) * SCALE_VALUE[q[1]][:, None, :, None] + 0.0).reshape(128, -1).astype(np.float32)
def f(rng, *shape):
    return mx_ref.flush((rng.standard_normal(shape, dtype=np.float32) * np.exp2(rng.integers(-2, 3, shape[:-1] + (1,)))).astype(BF))
def wide(rng, *shape, cols=0):
    v = rng.standard_normal(shape, dtype=np.float32) * np.exp2(rng.integers(-12, 13, shape)).astype(np.float32)
    if cols: v *= np.repeat(np.exp2(rng.integers(-cols, cols + 1, shape[:-2] + (1, shape[-1] // 4))) * (rng.random(shape[:-2] + (1, shape[-1] // 4)) > 0.0625), 4, axis=-1).astype(np.float32)
    return mx_ref.flush(v.astype(BF))
C, B, K, R = 512, 6, 64, 2
def key_of(s):
    b = (s.reshape(8, 16, C)[:, :B] < 0).astype(np.int64)
    return np.sum(b << np.arange(B)[:, None], axis=1)
def parts(t):
    return t.reshape(8, 16, -1, 4).transpose(0, 2, 1, 3)
def whole(p):
    return np.ascontiguousarray(p.transpose(0, 2, 1, 3)).reshape(128, -1)
def scan(p, key, start):
    h, o, g = np.array(start, np.float32), np.zeros((8, C, 16, 4), np.float32), np.arange(8)
    for j in range(C):
        n = np.maximum(np.float32(0.5) * h[g, key[:, j]], p[:, j])
        h[g, key[:, j]] = n
        o[:, j] = n
    return o, h
def same(a):
    return np.stack([a] * N)
def weights(rng, w):
    c, p = packed(same(w), rng)
    return {"wc": c, "ws": p}
def planted(rng, x, keys, size=np.ones((8, B)), swap=False, add=False, second=None):
    x[:, :, :8] = 0
    for e, k in ((0, keys),) if second is None else ((0, keys), (2, second)):
        for i in range(B):
            bit = k >> i & 1
            x[:, :, i, :, e] = (1 - bit).astype(np.float32).astype(BF)
            x[:, :, i, :, e + 1] = bit.astype(np.float32).astype(BF)
    u = np.zeros((128, 128, 4), np.float32)
    for g in range(8):
        for i in range(B):
            u[16 * g + i, 16 * g + i, 0] = size[g, i]
            u[16 * g + i, 16 * g + i, 1] = -size[g, i]
    w = np.zeros((128, 4, 128, 4), np.float32)
    i = np.arange(128)
    for b in range(4): w[i, b, i, b] = 32
    n = i[i % 16 < 8]
    turn = (1, 0, 2, 3) if swap else (0, 1, 2, 3) if second is None else (2, 3, 0, 1)
    for b in range(4):
        w[n, b, n, b] = 0
        w[n, b, n, turn[b]] = 32
    if add:
        n = i[(i % 16 >= 8) & (i % 16 < 12)]
        for b in range(4): w[n + 4, b, n, b] = 32
    return {"x": x.reshape(N, 128, 4 * C), "u": same(u.reshape(128, 512).astype(BF)), "v": same(np.array(f(rng, 128, 512))), **weights(rng, w.reshape(128, 2048).astype(BF))}
def numbers_of(rng):
    return np.array(f(rng, N, 128, 4 * C)).reshape(N, 8, 16, C, 4)
def three(rng, k, shape=(8, 4)):
    return rng.integers(4, 8, shape) * 2.0 ** k
def setup_inputs(rng):
    return {"x": np.array(f(rng, N, 128, 4 * C)), "u": same(np.array(f(rng, 128, 512))), "v": same(np.array(f(rng, 128, 512))), **weights(rng, np.array(f(rng, 128, 2048)))}
def setup_inputs_long(rng):
    r, j = np.arange(N)[:, None], np.arange(C)[None, :]
    a = rng.permutation(K)
    n = rng.integers(0, K, (N, C))
    third = 3 * rng.integers(0, K // 3, (N, C)) + (-r) % 3
    each = np.stack([rng.permutation(C) % K for i in range(N)])
    alone = np.where(j == rng.integers(0, 48, (N, 1)), 0, K - 1)
    p = [a[0], a[r + 1], a[N + 1 + r % 2], third, each, K - 1 - j * K // C, alone, np.where((r == 0) | (r == N - 1), n, a[N + 3])]
    keys = np.zeros((N, 8, C), int)
    heads = rng.permutation(8)
    for g, q in zip(heads, p): keys[:, g] = q
    first = keys.copy()
    x = numbers_of(rng)
    s = 65 + rng.integers(0, 2) - r * (80 // N)
    s[0] += 8
    for g, large in ((int(heads[0]), (C - 1 - j - s) % 80 == 0), (int(heads[6]), ((C - 1 - j) % 80 == 0) & (j >= 80))):
        first[:, g] = np.where(large, a[1], a[2])
        x[:, g, 8:, :, 2:] = three(rng, -30, (N, 8, C, 2)).astype(np.float32).astype(BF)
        x[:, g, 8:, :, :2] = np.where(large[:, None, :, None], three(rng, 27, (N, 8, C, 2)), 0.0).astype(np.float32).astype(BF)
        x[:, g, 8, :, 0] = np.where(large, 2.0 ** 30, 0.0).astype(np.float32).astype(BF)
    return planted(rng, x, first, second=keys)
def place_in_key(keys):
    o = np.argsort(keys, axis=-1, kind="stable")
    s = np.take_along_axis(keys, o, axis=-1)
    i = np.broadcast_to(np.arange(C), s.shape)
    head = np.ones(s.shape, bool)
    head[..., 1:] = s[..., 1:] != s[..., :-1]
    n = np.zeros(s.shape, int)
    np.put_along_axis(n, o, i - np.maximum.accumulate(np.where(head, i, 0), axis=-1), axis=-1)
    return n
def setup_inputs_near(rng):
    odd = rng.permutation(8) % 2
    size = np.exp2(np.where(odd, 28.0, -28.0))[:, None] * np.ones((8, B))
    low = rng.integers(0, B, 8)
    size[np.arange(8), low] = 0
    keys = rng.integers(0, K, (N, 8, C)) & ~(1 << low)[None, :, None]
    none = [rng.permutation(C)[:2] for r in range(N)]
    for r in range(N): keys[r][:, none[r]] = 0
    x = numbers_of(rng)
    m = (place_in_key(keys) % 2)[:, :, None, :, None]
    s = np.where(m == 0, 2.0, 1.0)
    up = (rng.integers(0, 2, (N, 8, 4, 1, 2)) + m) % 2
    x[:, :, 8:12, :, :2] = s.astype(np.float32).astype(BF)
    x[:, :, 12:, :, :2] = (s * (8 + up) * 2.0 ** -7).astype(np.float32).astype(BF)
    d = planted(rng, x, keys, size, add=True)
    x = d["x"].astype(np.float32).reshape(N, 8, 16, C, 4)
    for g in np.flatnonzero(odd == 0): x[:, g, :8] *= np.float32(2.0 ** -20)
    x = x.astype(BF).reshape(N, 128, C, 4)
    for r in range(N): x[r][:, none[r]] = 0
    return {**d, "x": x.reshape(N, 128, 4 * C)}
def setup_inputs_gone(rng):
    keys = 2 * rng.integers(0, K // 2, (N, 8, C)) + (np.arange(N)[:, None, None] + rng.integers(0, 2, (1, 8, 1))) % 2
    return planted(rng, numbers_of(rng), keys, swap=True)
def step(rng, v, n):
    return v * 2.0 ** -n + rng.choice([-1.0, 1.0], v.shape) * 2.0 ** (19 - n)
def runs(rng, t):
    v, s = three(rng, 20), [three(rng, -8) for i in range(4)]
    if t == 0: return [v] + s
    if t == 1: return s + [v]
    if t == 2: return [v, -2.0 * v] + s[:3]
    return [v] + [step(rng, v, n) for n in range(1, 5)]
def setup_inputs_order(rng):
    x = numbers_of(rng)
    keys = np.zeros((2, N, 8, C), int)
    def plant(r, g, j, k, v):
        keys[:, r, g, j] = k
        x[r, g, 8:, j] = v.astype(np.float32).astype(BF)
    firsts = rng.permutation(8) % (N - 3)
    for g in range(8):
        o = rng.permutation(K)
        keys[:, :, g] = o[9 + rng.integers(0, K - 9, (N, C))]
        at = [rng.permutation(C) for r in range(N)]
        for t in (0, 2):
            first = int(rng.integers(0, N - 1)) if g % 2 else 0
            v = three(rng, 20)
            plant(first, g, at[first][t], o[t], v)
            for r in range(first + 1, N): plant(r, g, at[r][t], o[t], three(rng, -8) if t == 0 else step(rng, v, r - first))
        a, b = 0, N - 1
        if g % 4:
            a = int(rng.integers(0, N - 2))
            b = int(rng.integers(a + 2, N))
        plant(a, g, at[a][1], o[1], three(rng, 20))
        plant(b, g, at[b][1], o[1], three(rng, -8))
        for t in range(4):
            for r in range(N):
                v = runs(rng, t)
                for i, j in enumerate(np.sort(at[r][3 + 5 * t:8 + 5 * t])): plant(r, g, j, o[3 + t], v[i])
        first = int(firsts[g])
        v = np.zeros((8, 4))
        v[7] = 11 * 2.0 ** (4 + rng.permutation([-1, 0, 0, 1]))
        plant(first, g, at[first][23], o[7], v)
        for r in range(first + 1, N):
            v = np.zeros((8, 4))
            v[:7] = three(rng, 20, (7, 4))
            plant(r, g, at[r][23], o[7], v)
            keys[0, r, g, at[r][23]] = o[8]
    return planted(rng, x, keys[0], second=keys[1])
def setup_inputs_spread(rng):
    d = setup_inputs(rng)
    x = wide(rng, N, 128, 4 * C).astype(np.float32) * np.repeat(np.exp2(rng.integers(-4, 5, (N, 1, C))), 4, axis=-1).astype(np.float32)
    d["x"] = np.array(mx_ref.flush(x.astype(BF)))
    return d
def check_inputs(d):
    b = []
    for k in ("x", "u", "v"):
        a = np.abs(d[k].astype(np.float32))
        if not (np.isfinite(a).all() and ((a == 0) | (a >= 2.0 ** -30) & (a <= 2.0 ** 30)).all()): b.append("a value of " + k)
    for k in ("u", "v"):
        a = d[k].astype(np.float32)
        if not (a == a[:1]).all(): b.append(k + " differs between ranks")
    if (d["wc"] != d["wc"][:1]).any(): b.append("wc differs between ranks")
    s = [mx_ref.live(p) for p in d["ws"]]
    if any((p != s[0]).any() for p in s): b.append("ws differs between ranks")
    if ((d["wc"] & 127) == 127).any(): b.append("a code of wc")
    a = np.max(np.abs(decode(pk(d["wc"][0], d["ws"][0]))).reshape(16, 8, -1, 4), axis=(1, 3))
    if not ((a == 0) | (a >= 2.0 ** -30) & (a <= 2.0 ** 30)).all(): b.append("a block of W")
    return b
def reference(x, u, v, wc, ws):
    w, qu, qv = pk(wc[0], ws[0]), mx_ref.quantize(u[0]), mx_ref.quantize(v[0])
    now = [mx_ref.quantize(x[r]) for r in range(N)]
    for t in range(R):
        p, key, last = [], [], []
        for r in range(N):
            key.append(key_of(mx_ref.matmul(qu, now[r])))
            made = tile([mx_ref.matmul(pick(w, np.arange(128 * b, 128 * b + 128)), now[r]) * np.float32(0.03125) for b in range(4)])
            p.append(parts(made.astype(np.float32)))
            h = scan(p[r], key[r], np.zeros((8, K, 16, 4), np.float32))[1]
            last.append(mx_ref.quantize(whole(h).astype(BF)))
        came = decode(join(*last))
        c, before = np.zeros((128, 4 * K), np.float32), []
        for r in range(N):
            before.append(mx_ref.quantize(c.astype(BF)))
            c = np.maximum(np.float32(0.5) * c, cut(came, r, 4 * K))
        start = decode(join(*before))
        for r in range(N):
            h = scan(p[r], key[r], parts(np.ascontiguousarray(cut(start, r, 4 * K))))[0]
            now[r] = mx_ref.quantize(whole(h).astype(BF))
    y = np.zeros((N, 128, C), np.float32)
    oc, osc = np.zeros((N, 128, 4 * C), np.uint8), np.zeros((N, 16, C), np.uint8)
    for r in range(N):
        y[r] = mx_ref.matmul(qv, now[r])
        oc[r], osc[r] = emit(now[r])
    return {"y": y, "oc": oc, "osc": osc}

@@ -1,0 +1,460 @@
+from concourse.bass import DstId, RemoteDMATransfer
+from concourse.mybir import dt, AluOpType as ALU, ActivationFunctionType as ACT
+
+N, C, K, R = 8, 512, 64, 2
+H = C // 2
+SL = C + K
+PW = C + 16
+WS, GS = 22, 20
+F, B, I, U = "float32", "bfloat16", "int32", "uint16"
+Q4, U8 = "float8_e4m3fn_x4", "uint8"
+
+
+def _sb(n, d):
+    return ("sbuf", [128, n], d)
+
+
+SCRATCH = {
+    "xt": _sb(4 * C, B), "ut": _sb(512, B), "vt": _sb(512, B),
+    "uq": _sb(128, Q4), "us": _sb(128, U8), "vq": _sb(128, Q4), "vs": _sb(128, U8),
+    "wq": _sb(512, Q4), "wp": _sb(512, U8), "iq": _sb(512 * (N - 1), Q4), "ip": _sb(512 * (N - 1), U8),
+    "aq0": _sb(C, Q4), "as0": _sb(C, U8), "aq1": _sb(C, Q4), "as1": _sb(C, U8), "aq2": _sb(C, Q4), "as2": _sb(C, U8),
+    "lq0": _sb(9 * K, Q4), "lp0": _sb(9 * K, U8), "lq1": _sb(9 * K, Q4), "lp1": _sb(9 * K, U8),
+    "cq": _sb(128, Q4), "cp": _sb(128, U8),
+    "pa": ("psum", [128, 2048], F), "pb": ("psum", [128, 2048], F),
+    "cb": _sb(136, F), "ct": _sb(128, F), "sc": _sb(8, F), "tb": _sb(256, F), "lc": _sb(64, U), "lr": _sb(144, U),
+    "ones": _sb(512, B), "eye": _sb(128, B), "id0": _sb(2048, B), "id1": _sb(2048, B),
+    "h8": _sb(256, B), "r16": _sb(512, B), "jf": _sb(C, B), "jw": _sb(32, F), "dm": _sb(SL, B),
+    "xp": _sb(544, B), "tt": _sb(1056, B), "bg": _sb(256, B), "kh": _sb(256, B), "tmp": _sb(32, F),
+    "wa": _sb(520, F), "wb": _sb(520, F), "wl": _sb(C, F), "wi": _sb(C, F), "acc": _sb(8, F),
+    "cum": _sb(1544, F), "x4": _sb(4, I), "y8": _sb(8, I),
+    "vv": _sb(C, F), "vt2": _sb(C, F), "vs2": _sb(C, F),
+    "y64": _sb(64, F), "yt": _sb(64, F), "z32": _sb(32, F), "zt": _sb(32, F), "zi": _sb(32, I), "za": _sb(32, I),
+    "fl0": _sb(SL, B), "fl1": _sb(SL, B), "dg": _sb(SL, "float16"), "mk0": _sb(SL, B), "mk1": _sb(SL, B),
+    "pp": _sb(4 * PW, B), "ps": _sb(4 * SL, B), "hs": _sb(4 * SL, B), "et": _sb(512, B), "cc": _sb(512, B),
+    "cs": _sb(4 * K, B), "ht": _sb(4 * C, B), "ysb": _sb(C, F),
+}
+SEMAPHORES = (["cv", "cs", "ct", "cg", "ls", "dx0", "dx1", "du", "dv", "dw", "dout", "dout2"]
+              + ["%s%d_%d" % (a, t, r) for a in "xof" for t in range(R) for r in range(N)])
+
+
+def rank_program(g, core, T, topo):
+    rank = T.rank_of(core)
+    if rank is None:
+        return
+    cores = list(T.cores)
+    eng = {"v": g.vector, "s": g.scalar, "t": g.tensor, "g": g, "y": g.sync}
+    own = {"v": "cv", "s": "cs", "t": "ct", "g": "cg"}
+    count = {}
+    known = {q: {} for q in eng}
+    writer, readers = {}, {}
+
+    def need(q, ev):
+        sem, n, _, kn = ev
+        if known[q].get(sem, 0) < n:
+            eng[q].wait_ge(T.sem[sem], n)
+            known[q][sem] = n
+        for s, m in kn.items():
+            if known[q].get(s, 0) < m:
+                known[q][s] = m
+
+    def order(q, rd, wr):
+        evs = []
+        for t in rd:
+            if t in writer:
+                evs.append(writer[t])
+            if t[0] == "@":
+                evs += [e for e in readers.get(t, []) if e[2] != q]
+        for t in wr:
+            if t in writer:
+                evs.append(writer[t])
+            evs += readers.get(t, [])
+        for e in sorted(evs, key=lambda e: -e[1]):
+            need(q, e)
+
+    def note(ev, rd, wr):
+        for t in rd:
+            readers.setdefault(t, []).append(ev)
+        for t in wr:
+            writer[t] = ev
+            readers[t] = []
+
+    def op(q, fn, rd, wr, sem=None, inc=1):
+        order(q, rd, wr)
+        sem = sem or own[q]
+        fn().then_inc(T.sem[sem], inc)
+        count[sem] = count.get(sem, 0) + inc
+        note((sem, count[sem], q, dict(known[q])), rd, wr)
+
+    def dma(q, out, in_, rd, wr, sem):
+        op(q, lambda: eng[q].dma_start(out, in_), rd, wr, sem, 16)
+
+    V, S, PE = g.vector, g.scalar, g.tensor
+
+    def ts(out, in0, s1, op0, rd, wr, s2=None, op1=None):
+        if op1 is None:
+            op("v", lambda: V.tensor_scalar(out, in0, s1, None, op0), rd, wr)
+        else:
+            op("v", lambda: V.tensor_scalar(out, in0, s1, s2, op0, op1), rd, wr)
+
+    def cp(q, out, in_, rd, wr):
+        if q == "v":
+            op("v", lambda: V.tensor_copy(out, in_), rd, wr)
+        else:
+            op("s", lambda: S.activation(out, in_, ACT.Copy), rd, wr)
+
+    def fill(ap, val, wr):
+        op("v", lambda: V.memset(ap, val), [], wr)
+
+    def iota(ap, pat, base, wr):
+        op("g", lambda: g.iota(ap, pat, base, 0, allow_small_or_imprecise_dtypes=True), [], wr)
+
+    def scan(out, d0, d1, init, op0, op1, rd, wr):
+        op("v", lambda: V.tensor_tensor_scan(out, d0, d1, init, op0, op1), rd, wr)
+
+    def tr(out, in_, rd, wr):
+        op("v", lambda: V.transpose(out, in_), rd, wr)
+
+    def quant(q, s, in_, rd, wr):
+        op("v", lambda: V.quantize_mx(q, s, in_), rd, wr)
+
+    def mm(out, lq, ls, rq, rs, rd, wr):
+        op("t", lambda: PE.matmul_mx(out, lq, ls, rq, rs, True, True), rd, wr)
+
+    def bank(name, b, lo, hi):
+        return T[name][:, 512 * b + lo:512 * b + hi]
+
+    chips = [topo.chip(c) for c in cores]
+    first = [r for r in range(N) if chips[r] == chips[0]]
+    second = [r for r in range(N) if chips[r] != chips[0]]
+    taker = {r: second[min(i, len(second) - 2)] for i, r in enumerate(first)}
+
+    def pieces(r):
+        if r in first:
+            return [], [], list(range(r))
+        return ([i for i in first[1:] + first[:1] if taker[i] != r], [i for i in first if taker[i] == r],
+                [i for i in second if i < r])
+
+    def slot(r, i):
+        a, b, c = pieces(r)
+        return (a + b + c + [r]).index(i)
+
+    def bits(m):
+        return bin(m).count("1")
+
+    def far_mask(r):
+        return topo.mask(cores[r], cores[taker[r]])
+
+    def near_mask(r):
+        other = [i for i in range(N) if chips[i] == chips[r] and i != r][0]
+        m = topo.mask(cores[r], cores[other])
+        return m & ~far_mask(r) if r in first else m
+
+    def plan(r):
+        to = [i for i in range(N - 1, r, -1) if chips[i] == chips[r]]
+        if r not in first:
+            return [[(to, near_mask(r), "o")]] if to else []
+        calls = [[([taker[r]], far_mask(r), "x")] + ([(to[:2], near_mask(r), "o")] if to else [])]
+        return calls + ([[(to[2:], far_mask(r), "o")]] if to[2:] else [])
+
+    def dst(r):
+        a = topo.addr(cores[r])
+        return DstId(rid=a[0], pnc=a[1])
+
+    def send(t, groups, rd):
+        order("g", rd, [])
+        for name, wide in (("lq%d" % t, True), ("lp%d" % t, False)):
+            def view(r, i, n):
+                a = T[name][:, K * slot(r, i):K * (slot(r, i) + n)]
+                return a.bitcast(dt.uint8) if wide else a
+            trs = [RemoteDMATransfer(dst_ids=[dst(r) for r in to], dma_engine_mask=m, remote_sem=T.sem[sem],
+                                     src=view(rank, i, n), dsts=[view(r, i, n) for r in to])
+                   for i, n, to, m, sem in groups]
+            g.remote_dma_fused(trs, local_sem=T.sem.ls)
+            count["ls"] = count.get("ls", 0) + sum(bits(x[3]) for x in groups)
+
+    handed, across, near = pieces(rank)
+    for t in range(R):
+        for i in handed:
+            writer["L%d_%d" % (t, slot(rank, i))] = ("f%d_%d" % (t, taker[i]), 2 * bits(near_mask(taker[i])), None, {})
+        for i in across + near:
+            m, kind = [(m, kind) for call in plan(i) for to, m, kind in call if rank in to][0]
+            writer["L%d_%d" % (t, slot(rank, i))] = ("%s%d_%d" % (kind, t, i), 2 * bits(m), None, {})
+    last = rank == N - 1
+
+    dma("y", T.xt[:, 0:4 * H], T.x[:, 0:4 * H], [], ["xt0"], "dx0")
+    dma("s", T.ut[:], T.u[:], [], ["ut"], "du")
+    dma("y", T.xt[:, 4 * H:4 * C], T.x[:, 4 * H:4 * C], [], ["xt1"], "dx1")
+    order("y", ["xt1"], [])
+    dma("y", T.wq[:].bitcast(dt.uint8), T.wc[:], [], [], "dw")
+    dma("y", T.wp[:], T.ws[:], [], ["w"], "dw")
+    dma("y", T.vt[:], T.v[:], [], ["vt"], "dv")
+
+    cb, ct, sc, tb, lc, lr = T.cb, T.ct, T.sc, T.tb, T.lc, T.lr
+    iota(cb[:, 64:80], [[544, 2], [-1, 8]], 7, ["cb2"])
+    iota(cb[:, 80:96], [[-512, 2], [-1, 8]], 535, ["cb3"])
+    iota(cb[:, 0:32], [[0, 2], [1, 16]], 0, ["cb0"])
+    iota(cb[:, 32:64], [[1, 32]], 0, ["cb1"])
+    iota(cb[:, 96:128], [[0, 2], [1, 8], [16, 2]], 0, ["cb4"])
+    iota(cb[:, 128:132], [[16, 2], [0, 2]], 15, ["cb5"])
+    iota(T.cum[:, 513:1024], [[0, 511]], 0, ["gap"])
+    fill(T.ones[:], 1.0, ["ones"])
+    op("g", lambda: g.affine_select(T.r16[:], T.ones[:], [[0, 32], [1, 16]], ALU.not_equal, 0.0, 0, 0), ["ones"], ["r16"])
+    iota(T.jf[:], [[1, C]], -H, ["jf"])
+    iota(T.fl0[:], [[0, SL]], H, ["fl0"])
+    if rank:
+        op("g", lambda: g.affine_select(T.eye[:], T.ones[:, 0:128], [[-1, 128]], ALU.is_equal, 0.0, 0, 1), ["ones"], ["eye"])
+        for i in range(min(rank, 2)):
+            iota(T["id%d" % i][:], [[0, 2048]], 0, ["id%d" % i])
+    fill(T.h8[:], 2.0, ["h8"])
+    fill(T.xp[:, 0:16], 0.0, ["xpa"])
+    fill(T.xp[:, 528:544], 0.0, ["xpb"])
+    fill(tb[:, 0:80], 0.0, ["tz"])
+    for i in range(3):
+        op("v", lambda: V.memset(T.h8[:, i:256:8], 0.0), ["h8"], ["h8_%d" % i])
+    fill(T.pp[:, C:4 * PW:PW], 0.0, ["pz"])
+    fill(T.wb[:, 0:1], 2049.0, ["wb0"])
+    fill(T.et[:, 256:512], 0.0, ["epad"])
+    fill(T.cc[:, 256:512], 0.0, ["cpad"])
+    tr(ct[:], cb[:, 0:128], ["cb0", "cb1", "cb2", "cb3", "cb4"], ["ct"])
+    q, rr, kk, fin = ct[:, 0:1], ct[:, 32:33], ct[:, 64:65], ct[:, 96:97]
+    row, k16 = cb[:, 32:64], cb[:, 0:32]
+    GB, G64, G32, GF, GQ = lc[:, 0:16], lc[:, 16:20], lc[:, 20:22], lc[:, 22:24], lc[:, 24:60]
+    KW, LS, L1, L2, HD, TL = lr[:, 0:32], lr[:, 32:64], lr[:, 64:96], lr[:, 96:132], lr[:, 132:136], lr[:, 136:140]
+    ts(GB, cb[:, 32:48], 32.0, ALU.mult, ["ct"], ["GB"], kk, ALU.add)
+    ts(tb[:, 16:32], cb[:, 0:16], q, ALU.is_equal, ["ct", "tz"], ["tz1"])
+    ts(tb[:, 48:64], cb[:, 0:16], q, ALU.is_equal, ["ct", "tz"], ["tz2"], 2048.0, ALU.mult)
+    ts(tb[:, 144:176], k16, q, ALU.is_lt, ["ct"], ["tl1"], 2048.0, ALU.add)
+    ts(tb[:, 176:208], k16, q, ALU.is_lt, ["ct"], ["tl2"], 2048.0, ALU.mult)
+    ts(tb[:, 80:112], k16, q, ALU.is_equal, ["ct"], ["ti1"])
+    ts(tb[:, 112:144], k16, q, ALU.is_equal, ["ct"], ["ti2"], 1.0 / 2048, ALU.mult)
+    ts(T.wa[:, 0:1], q, 4098.0, ALU.mult, ["ct"], ["wa0"], 65536.0, ALU.add)
+    ts(sc[:, 0:1], q, 32.0, ALU.mult, ["ct"], ["sc0"])
+    ts(sc[:, 1:2], q, 15.0, ALU.is_equal, ["ct"], ["sc1"], 1024.0, ALU.mult)
+    ts(sc[:, 2:3], q, 1.0, ALU.add, ["ct"], ["sc2"], 1.0 / 16, ALU.mult)
+    ts(sc[:, 3:4], q, 1.0, ALU.add, ["ct"], ["sc3"])
+    ts(G32, cb[:, 32:34], 32.0, ALU.mult, ["ct"], ["G32"], rr, ALU.add)
+    ts(GF, cb[:, 32:34], 8.0, ALU.mult, ["ct"], ["GF"], fin, ALU.add)
+    ts(G64, cb[:, 128:132], sc[:, 0:1], ALU.add, ["cb5", "sc0"], ["G64"])
+    ts(T.jw[:], row, sc[:, 2:3], ALU.add, ["sc2"], ["jw"], 1.0 / 64, ALU.mult)
+    quant(T.uq[:], T.us[:], T.ut[:], ["ut"], ["u"])
+    ts(GQ, cb[:, 0:36], 0.0, ALU.mult, ["ct"], ["GQ"], q, ALU.add)
+    ts(tb[:, 208:224], cb[:, 0:16], q, ALU.is_equal, ["ct"], ["tm1"], -4096.0, ALU.mult)
+    ts(tb[:, 224:240], cb[:, 0:16], sc[:, 3:4], ALU.is_equal, ["sc3"], ["tm2"], 1024.0, ALU.mult)
+    op("v", lambda: V.tensor_tensor(tb[:, 240:256], tb[:, 208:224], tb[:, 224:240], ALU.add), ["tm1", "tm2"], ["tm"])
+    cp("s", T.dm[:], tb[:, 240:256].indirect(GQ), ["tm", "GQ"], ["dm"])
+    for t in range(R):
+        op("s", lambda: S.activation(T["mk%d" % t][:], T.dm[:], ACT.Identity, 0.5, 0.0), ["dm"], ["mk%d" % t])
+
+    def state(t, tile, h, rd):
+        quant(T["aq%d" % t][:, H * h:H * h + H], T["as%d" % t][:, H * h:H * h + H],
+              tile[:, 4 * H * h:4 * H * (h + 1)], rd, ["a%d_%d" % (t, h)])
+
+    def signs(t, h):
+        mm(bank("pb", h, 0, H), T.uq[:], T.us[:], T["aq%d" % t][:, H * h:H * h + H], T["as%d" % t][:, H * h:H * h + H],
+           ["u", "a%d_%d" % (t, h)], ["@b%d" % h])
+
+    def minus(h):
+        ts(T.xp[:, 16 + H * h:16 + H * h + H], bank("pb", h, 0, H), 0.0, ALU.is_lt, ["@b%d" % h], ["xp%d" % h])
+
+    def plane(b):
+        op("s", lambda: S.activation(T.pp[:, PW * b:PW * b + C], bank("pa", b, 0, C), ACT.Copy, scale=0.03125),
+           ["@a%d" % b], ["p%d" % b])
+
+    def unit(e):
+        for b in range(4):
+            tok = "id%d" % (e % 2)
+            op("s", lambda: S.activation(T[tok][:, 513 * b:512 * b + 512:4], T.eye[:], ACT.Copy, scale=0.5 ** e),
+               ["eye", tok], [tok + str(b)])
+
+    state(0, T.xt, 0, ["xt0"])
+    signs(0, 0)
+    minus(0)
+    state(0, T.xt, 1, ["xt1"])
+
+    for t in range(R):
+        aq, ap = T["aq%d" % t], T["as%d" % t]
+        a0, a1 = "a%d_0" % t, "a%d_1" % t
+        fl, mk, flt, mkt = T["fl%d" % t], T["mk%d" % t], "fl%d" % t, "mk%d" % t
+        lq, lp = T["lq%d" % t], T["lp%d" % t]
+        for h in range(0 if t else 1, 2):
+            signs(t, h)
+        for b in range(4):
+            mm(bank("pa", b, 0, C), T.wq[:, 128 * b:128 * b + 128], T.wp[:, 128 * b:128 * b + 128], aq[:], ap[:],
+               ["w", a0, a1], ["@a%d" % b])
+        if t:
+            minus(0)
+            plane(0)
+        tr(T.tt[:, 0:H], T.xp[:, 16:16 + H], ["xp0"], ["t0"])
+        tr(T.tt[:, C:C + H], T.xp[:, 0:H], ["xp0", "xpa"], ["t1"])
+        minus(1)
+        tr(T.tt[:, H:C], T.xp[:, 16 + H:16 + C], ["xp1"], ["t2"])
+        tr(T.tt[:, C + H:1056], T.xp[:, H:544], ["xp0", "xp1", "xpb"], ["t3"])
+        cp("v", T.bg[:], T.tt[:, 0:1056].indirect(GB), ["t0", "t1", "t2", "t3", "GB"], ["bg"])
+        scan(T.kh[:], T.h8[:], T.bg[:], 0.0, ALU.mult, ALU.add, ["bg", "h8_0", "h8_1", "h8_2"], ["kh"])
+        cp("v", KW, T.kh[:, 7:256:8], ["kh"], ["KW"])
+        op("s", lambda: S.activation(T.wl[:], tb[:, 144:208].indirect(KW), ACT.Copy, accum_out=T.acc[:, 0:1]),
+           ["KW", "tl1", "tl2"], ["acc", "wl"])
+        cp("v", T.wa[:, 1:C + 1], tb[:, 16:80].indirect(KW), ["KW", "tz", "tz1", "tz2"], ["wa"])
+        cp("s", T.wb[:, 1:C + 1], tb[:, 0:64].indirect(KW), ["KW", "tz", "tz1", "tz2"], ["wb"])
+        cp("s", T.wi[:, 0:16 * WS], tb[:, 80:144].indirect(lr[:, 0:WS]), ["KW", "ti1", "ti2"], ["wi"])
+        op("v", lambda: V.tensor_tensor(T.tmp[:], T.bg[:, 3:256:8], T.jw[:], ALU.add), ["bg", "jw"], ["tmp"])
+        scan(T.cum[:, 0:C + 1], T.wa[:, 0:C + 1], T.wa[:, 0:C + 1], T.acc[:, 0:1], ALU.add, ALU.max,
+             ["wa", "wa0", "acc"], ["cumA"])
+        ts(LS, T.tmp[:], 1024.0, ALU.mult, ["tmp"], ["LS"])
+        cp("v", T.wi[:, 16 * WS:C], tb[:, 80:144].indirect(lr[:, WS:32]), ["KW", "ti1", "ti2"], ["wi2"])
+        scan(T.cum[:, 1024:1024 + C + 1], T.wb[:, 0:C + 1], T.wb[:, 0:C + 1], T.cum[:, C:C + 1], ALU.add, ALU.max,
+             ["wb", "wb0", "cumA"], ["cumB"])
+        for b in range(1 if t else 0, 4):
+            plane(b)
+        if t == 0 and rank:
+            unit(0)
+        op("v", lambda: V.tensor_tensor(T.vv[:], T.cum[:, 0:1537].indirect(LS), T.wi[:], ALU.mult),
+           ["cumA", "cumB", "gap", "LS", "wi", "wi2"], ["vv"])
+        cp("v", T.x4[:], T.cum[:, 0:1537:512], ["cumA", "cumB"], ["x4"])
+        tr(T.vt2[:], T.vv[:], ["vv"], ["vt2"])
+        ts(T.y8[:, 0:4], T.x4[:], 2047, ALU.bitwise_and, ["x4"], ["y8a"])
+        scan(T.vs2[:], T.r16[:], T.vt2[:], 0.0, ALU.mult, ALU.add, ["vt2", "r16"], ["vs2"])
+        ts(T.y8[:, 4:8], T.x4[:], 11, ALU.logical_shift_right, ["x4"], ["y8b"])
+        cp("v", T.y64[:], T.vs2[:].indirect(G64), ["vs2", "G64"], ["y64"])
+        cp("v", HD, T.y8[:, 0:8:2], ["y8a", "y8b"], ["HD"])
+        tr(T.yt[:], T.y64[:], ["y64"], ["yt"])
+        cp("v", TL, T.y8[:, 1:8:2], ["y8a", "y8b"], ["TL"])
+        cp("v", T.z32[:], T.yt[:].indirect(G32), ["yt", "G32"], ["z32"])
+        tr(T.zt[:], T.z32[:], ["z32"], ["zt"])
+        cp("v", T.zi[:], T.zt[:].indirect(GF), ["zt", "GF"], ["zi"])
+        ts(T.za[:], T.zi[:], 2047, ALU.bitwise_and, ["zi"], ["za"])
+        cp("v", L1, T.za[:], ["za"], ["L1"])
+        cp("v", fl[:].indirect(L1), T.jf[:], ["L1", "jf"], [flt])
+        scan(T.dg[:], T.dm[:], fl[:], 0.0, ALU.add, ALU.max, ["dm", flt], ["dg"])
+        ts(L2, T.dg[:, 15:SL:16], sc[:, 1:2], ALU.add, ["dg", "sc1"], ["L2"], float(H - 1024), ALU.add)
+
+        def srt(q_, b, lo=0, hi=SL // 16, part=""):
+            cp(q_, T.ps[:, SL * b + 16 * lo:SL * b + 16 * hi],
+               T.pp[:, PW * b:PW * b + C + 1].indirect(lr[:, 96 + lo:96 + hi]),
+               ["L2", "pz", "p%d" % b], ["s%d%s" % (b, part)])
+
+        def run(b):
+            scan(T.hs[:, SL * b:SL * b + SL], mk[:], T.ps[:, SL * b:SL * b + SL], 0.0, ALU.mult, ALU.max,
+                 [mkt, "s%d" % b, "s%dx" % b], ["h%d" % b])
+
+        def tail(q_, b):
+            cp(q_, T.et[:, b:256:4], T.hs[:, SL * b:SL * b + SL].indirect(TL), ["TL", "h%d" % b], ["e%d" % b])
+
+        def back(q_, b, lo=0, hi=2):
+            cp(q_, T.ht[:, 4 * H * lo + b:4 * H * hi:4],
+               T.hs[:, SL * b:SL * b + SL].indirect(lr[:, 64 + 16 * lo:64 + 16 * hi]),
+               ["L1", "h%d" % b], ["ht%d_%d" % (b, h) for h in range(lo, hi)])
+
+        def hand_on():
+            send(t, [(across[0], len(across), [r for r in second if r != rank], near_mask(rank),
+                      "f%d_%d" % (t, rank))], ["L%d_%d" % (t, slot(rank, i)) for i in across])
+
+        early = t > 0 and across == first[:1]
+        if early:
+            hand_on()
+        srt("s", 1)
+        srt("s", 2)
+        srt("s", 3, 0, GS)
+        srt("v", 0)
+        cp("v", mk[:].indirect(HD), T.et[:, 256:256 + K], ["HD", "epad"], [mkt])
+        srt("v", 3, GS, SL // 16, "x")
+        if not last:
+            for b in range(4):
+                run(b)
+            for b in range(4):
+                tail("sssv"[b], b)
+            s0 = slot(rank, rank)
+            mine = "L%d_%d" % (t, s0)
+            quant(lq[:, K * s0:K * s0 + 128], lp[:, K * s0:K * s0 + 128], T.et[:],
+                  ["e0", "e1", "e2", "e3", "epad"], [mine])
+            for call in plan(rank):
+                send(t, [(rank, 1, to, m, "%s%d_%d" % (kind, t, rank)) for to, m, kind in call], [mine])
+        if t == 0:
+            iota(T.fl1[:], [[0, SL]], H, ["fl1"])
+        if across and not early:
+            hand_on()
+        if t == 0:
+            for e in range(rank):
+                tok = "id%d" % (e % 2)
+                if e:
+                    unit(e)
+                quant(T.iq[:, 512 * e:512 * e + 512], T.ip[:, 512 * e:512 * e + 512], T[tok][:],
+                      [tok + str(b) for b in range(4)], ["i%d" % e])
+        if t == R - 1:
+            quant(T.vq[:], T.vs[:], T.vt[:], ["vt"], ["v"])
+
+        def unpack(nm, e, cq_, cp_, rd):
+            for b in range(4):
+                o = 512 * e + 128 * b
+                mm(bank("p" + nm, b, 0, 128), T.iq[:, o:o + 128], T.ip[:, o:o + 128], cq_, cp_,
+                   ["i%d" % e] + rd, ["@%s%d" % (nm, b)])
+
+        if rank:
+            soon = [i for i in handed if i == first[0]]
+            seq = (soon + across + near if t else near + across + soon) + [i for i in handed if i not in soon]
+            if rank in first:
+                seq = near[::-1]
+            cct = ["c%d" % b for b in range(4)]
+            have = [] if last else [rank]
+            for n, i in enumerate(seq):
+                sl = slot(rank, i)
+                there = [slot(rank, j) for j in have]
+                lo = sl - 1 if (sl - 1 in there and sl + 1 not in there) else sl
+                have.append(i)
+                nm = "ba"[n % 2]
+                unpack(nm, rank - 1 - i, lq[:, K * lo:K * lo + 128], lp[:, K * lo:K * lo + 128],
+                       ["L%d_%d" % (t, lo), "L%d_%d" % (t, lo + 1)])
+                o = K * (sl - lo)
+                for b in range(4):
+                    src, out = bank("p" + nm, b, o, o + K), T.cc[:, b:256:4]
+                    if n == 0:
+                        cp("v", out, src, ["@%s%d" % (nm, b)], [cct[b]])
+                    else:
+                        op("v", lambda: V.tensor_tensor(out, src, out, ALU.max), ["@%s%d" % (nm, b), cct[b]], [cct[b]])
+            quant(T.cq[:], T.cp[:], T.cc[:], cct + ["cpad"], ["cq"])
+            nm = "ba"[len(seq) % 2]
+            unpack(nm, 0, T.cq[:], T.cp[:], ["cq"])
+            for b in range(4):
+                cp("s" if b else "v", T.cs[:, K * b:K * b + K], bank("p" + nm, b, 0, K), ["@%s%d" % (nm, b)], ["cs%d" % b])
+
+            def head(b):
+                cp("v", T.ps[:, SL * b:SL * b + SL].indirect(HD), T.cs[:, K * b:K * b + K], ["HD", "cs%d" % b],
+                   ["s%d" % b, "s%dx" % b])
+            head(0)
+            run(0)
+            head(1)
+            head(2)
+            run(1)
+            head(3)
+            run(2)
+            run(3)
+            back("s", 0)
+            back("s", 1)
+            if t < R - 1:
+                back("s", 2)
+                back("v", 3)
+        else:
+            for b in range(4 if t < R - 1 else 2):
+                back("sv"[b % 2], b)
+        for h in range(2):
+            if t == R - 1:
+                back("s", 2, h, h + 1)
+                back("v", 3, h, h + 1)
+            state(t + 1, T.ht, h, ["ht%d_%d" % (b, h) for b in range(4)])
+
+    aq, ap = T["aq%d" % R], T["as%d" % R]
+    an = ["a%d_%d" % (R, h) for h in range(2)]
+    for h in range(2):
+        mm(bank("pa", h, 0, H), T.vq[:], T.vs[:], aq[:, H * h:H * h + H], ap[:, H * h:H * h + H], ["v", an[h]], ["@a%d" % h])
+        dma("y", T.oc[:, 4 * H * h:4 * H * (h + 1)], aq[:, H * h:H * h + H].bitcast(dt.uint8), [an[h]], [], "dout")
+    cp("s", T.ysb[:, 0:H], bank("pa", 0, 0, H), ["@a0"], ["y0"])
+    cp("v", T.ysb[:, H:C], bank("pa", 1, 0, H), ["@a1"], ["y1"])
+    dma("s", T.y[:, 0:H], T.ysb[:, 0:H], ["y0"], [], "dout2")
+    for k in range(4):
+        dma("s", T.osc[4 * k:4 * k + 4, :], ap[32 * k:32 * k + 4, :], an, [], "dout2")
+    dma("y", T.y[:, H:C], T.ysb[:, H:C], ["y1"], [], "dout")
+    for sem in ("cv", "cs", "ct", "cg", "dv", "dw", "dout", "dout2"):
+        g.sync.wait_ge(T.sem[sem], count[sem])
+    if "ls" in count:
+        g.wait_ge(T.sem.ls, count["ls"])

@@ -6,6 +6,7 @@ H = C // 2
 SL = C + K
 PW = C + 16
 WS, GS = 22, 20
+PART = ((0, H), (H, H + 128), (H + 128, C))
 F, B, I, U = "float32", "bfloat16", "int32", "uint16"
 Q4, U8 = "float8_e4m3fn_x4", "uint8"
 
@@ -22,20 +23,21 @@ SCRATCH = {
     "lq0": _sb(9 * K, Q4), "lp0": _sb(9 * K, U8), "lq1": _sb(9 * K, Q4), "lp1": _sb(9 * K, U8),
     "cq": _sb(128, Q4), "cp": _sb(128, U8),
     "pa": ("psum", [128, 2048], F), "pb": ("psum", [128, 2048], F),
-    "cb": _sb(136, F), "ct": _sb(128, F), "sc": _sb(8, F), "tb": _sb(256, F), "lc": _sb(64, U), "lr": _sb(144, U),
+    "cb": _sb(200, F), "ct": _sb(96, F), "kb": _sb(96, F), "kt": _sb(96, F),
+    "sc": _sb(8, F), "tb": _sb(256, F), "lc": _sb(64, U), "lr": _sb(144, U),
     "ones": _sb(512, B), "eye": _sb(128, B), "id0": _sb(2048, B), "id1": _sb(2048, B),
-    "h8": _sb(256, B), "r16": _sb(512, B), "jf": _sb(C, B), "jw": _sb(32, F), "dm": _sb(SL, B),
-    "xp": _sb(544, B), "tt": _sb(1056, B), "bg": _sb(256, B), "kh": _sb(256, B), "tmp": _sb(32, F),
+    "h6": _sb(192, B), "r16": _sb(512, B), "jf": _sb(C, B), "jw": _sb(32, F), "dm": _sb(SL, B),
+    "xp": _sb(544, B), "tt": _sb(1056, B), "bg": _sb(192, B), "kh": _sb(192, B), "tmp": _sb(32, F),
     "wa": _sb(520, F), "wb": _sb(520, F), "wl": _sb(C, F), "wi": _sb(C, F), "acc": _sb(8, F),
     "cum": _sb(1544, F), "x4": _sb(4, I), "y8": _sb(8, I),
     "vv": _sb(C, F), "vt2": _sb(C, F), "vs2": _sb(C, F),
-    "y64": _sb(64, F), "yt": _sb(64, F), "z32": _sb(32, F), "zt": _sb(32, F), "zi": _sb(32, I), "za": _sb(32, I),
+    "y64": _sb(64, F), "yt": _sb(64, F), "z32": _sb(32, I), "zt": _sb(32, I), "za": _sb(32, I),
     "fl0": _sb(SL, B), "fl1": _sb(SL, B), "dg": _sb(SL, "float16"), "mk0": _sb(SL, B), "mk1": _sb(SL, B),
     "pp": _sb(4 * PW, B), "ps": _sb(4 * SL, B), "hs": _sb(4 * SL, B), "et": _sb(512, B), "cc": _sb(512, B),
     "cs": _sb(4 * K, B), "ht": _sb(4 * C, B), "ysb": _sb(C, F),
 }
 SEMAPHORES = (["cv", "cs", "ct", "cg", "ls", "dx0", "dx1", "du", "dv", "dw", "dout", "dout2"]
-              + ["%s%d_%d" % (a, t, r) for a in "xof" for t in range(R) for r in range(N)])
+              + ["%s%d_%d" % (a, t, r) for a in ("x", "xs", "o", "f") for t in range(R) for r in range(N)])
 
 
 def rank_program(g, core, T, topo):
@@ -127,7 +129,7 @@ def rank_program(g, core, T, topo):
     chips = [topo.chip(c) for c in cores]
     first = [r for r in range(N) if chips[r] == chips[0]]
     second = [r for r in range(N) if chips[r] != chips[0]]
-    taker = {r: second[min(i, len(second) - 2)] for i, r in enumerate(first)}
+    taker = {r: second[max(len(second) - 2 - i, 0)] for i, r in enumerate(first)}
 
     def pieces(r):
         if r in first:
@@ -161,42 +163,49 @@ def rank_program(g, core, T, topo):
         a = topo.addr(cores[r])
         return DstId(rid=a[0], pnc=a[1])
 
-    def send(t, groups, rd):
-        order("g", rd, [])
-        for name, wide in (("lq%d" % t, True), ("lp%d" % t, False)):
+    def send(t, groups, have):
+        for name, wide in (("lp%d" % t, False), ("lq%d" % t, True)):
+            order("g", ["%s%d_%d" % ("L" if wide else "M", t, slot(rank, i)) for i in have], [])
+
             def view(r, i, n):
                 a = T[name][:, K * slot(r, i):K * (slot(r, i) + n)]
                 return a.bitcast(dt.uint8) if wide else a
-            trs = [RemoteDMATransfer(dst_ids=[dst(r) for r in to], dma_engine_mask=m, remote_sem=T.sem[sem],
+            trs = [RemoteDMATransfer(dst_ids=[dst(r) for r in to], dma_engine_mask=m,
+                                     remote_sem=T.sem["%s%d_%d" % ("xs" if kind == "x" and not wide else kind, t, rank)],
                                      src=view(rank, i, n), dsts=[view(r, i, n) for r in to])
-                   for i, n, to, m, sem in groups]
+                   for i, n, to, m, kind in groups]
             g.remote_dma_fused(trs, local_sem=T.sem.ls)
             count["ls"] = count.get("ls", 0) + sum(bits(x[3]) for x in groups)
 
     handed, across, near = pieces(rank)
     for t in range(R):
-        for i in handed:
-            writer["L%d_%d" % (t, slot(rank, i))] = ("f%d_%d" % (t, taker[i]), 2 * bits(near_mask(taker[i])), None, {})
-        for i in across + near:
-            m, kind = [(m, kind) for call in plan(i) for to, m, kind in call if rank in to][0]
-            writer["L%d_%d" % (t, slot(rank, i))] = ("%s%d_%d" % (kind, t, i), 2 * bits(m), None, {})
+        for i in handed + across + near:
+            if i in handed:
+                evs = [("f%d_%d" % (t, taker[i]), 2 * bits(near_mask(taker[i])), None, {})] * 2
+            else:
+                m, kind = [(m, kind) for call in plan(i) for to, m, kind in call if rank in to][0]
+                evs = [("o%d_%d" % (t, i), 2 * bits(m), None, {})] * 2
+                if kind == "x":
+                    evs = [("x%d_%d" % (t, i), bits(m), None, {}), ("xs%d_%d" % (t, i), bits(m), None, {})]
+            writer["L%d_%d" % (t, slot(rank, i))], writer["M%d_%d" % (t, slot(rank, i))] = evs
     last = rank == N - 1
 
-    dma("y", T.xt[:, 0:4 * H], T.x[:, 0:4 * H], [], ["xt0"], "dx0")
+    cut = 4 * PART[2][0]
+    dma("y", T.xt[:, 0:cut], T.x[:, 0:cut], [], ["xt0"], "dx0")
     dma("s", T.ut[:], T.u[:], [], ["ut"], "du")
-    dma("y", T.xt[:, 4 * H:4 * C], T.x[:, 4 * H:4 * C], [], ["xt1"], "dx1")
-    order("y", ["xt1"], [])
+    dma("y", T.xt[:, cut:4 * C], T.x[:, cut:4 * C], [], ["xt1"], "dx1")
+    order("y", ["xt0", "xt1"], [])
     dma("y", T.wq[:].bitcast(dt.uint8), T.wc[:], [], [], "dw")
     dma("y", T.wp[:], T.ws[:], [], ["w"], "dw")
     dma("y", T.vt[:], T.v[:], [], ["vt"], "dv")
 
     cb, ct, sc, tb, lc, lr = T.cb, T.ct, T.sc, T.tb, T.lc, T.lr
-    iota(cb[:, 64:80], [[544, 2], [-1, 8]], 7, ["cb2"])
-    iota(cb[:, 80:96], [[-512, 2], [-1, 8]], 535, ["cb3"])
     iota(cb[:, 0:32], [[0, 2], [1, 16]], 0, ["cb0"])
     iota(cb[:, 32:64], [[1, 32]], 0, ["cb1"])
-    iota(cb[:, 96:128], [[0, 2], [1, 8], [16, 2]], 0, ["cb4"])
-    iota(cb[:, 128:132], [[16, 2], [0, 2]], 15, ["cb5"])
+    iota(cb[:, 64:96], [[0, 2], [1, 8], [16, 2]], 0, ["cb2"])
+    iota(cb[:, 96:144], [[32, 4], [544, 2], [-1, 6]], 5, ["cb3"])
+    iota(cb[:, 144:192], [[32, 4], [-512, 2], [-1, 6]], 533, ["cb4"])
+    iota(cb[:, 192:196], [[16, 2], [0, 2]], 15, ["cb5"])
     iota(T.cum[:, 513:1024], [[0, 511]], 0, ["gap"])
     fill(T.ones[:], 1.0, ["ones"])
     op("g", lambda: g.affine_select(T.r16[:], T.ones[:], [[0, 32], [1, 16]], ALU.not_equal, 0.0, 0, 0), ["ones"], ["r16"])
@@ -206,22 +215,24 @@ def rank_program(g, core, T, topo):
         op("g", lambda: g.affine_select(T.eye[:], T.ones[:, 0:128], [[-1, 128]], ALU.is_equal, 0.0, 0, 1), ["ones"], ["eye"])
         for i in range(min(rank, 2)):
             iota(T["id%d" % i][:], [[0, 2048]], 0, ["id%d" % i])
-    fill(T.h8[:], 2.0, ["h8"])
+    fill(T.h6[:], 2.0, ["h6"])
     fill(T.xp[:, 0:16], 0.0, ["xpa"])
     fill(T.xp[:, 528:544], 0.0, ["xpb"])
     fill(tb[:, 0:80], 0.0, ["tz"])
-    for i in range(3):
-        op("v", lambda: V.memset(T.h8[:, i:256:8], 0.0), ["h8"], ["h8_%d" % i])
+    fill(T.h6[:, 0:192:6], 0.0, ["h6"])
     fill(T.pp[:, C:4 * PW:PW], 0.0, ["pz"])
     fill(T.wb[:, 0:1], 2049.0, ["wb0"])
+    tr(ct[:], cb[:, 0:96], ["cb0", "cb1", "cb2"], ["ct"])
     fill(T.et[:, 256:512], 0.0, ["epad"])
     fill(T.cc[:, 256:512], 0.0, ["cpad"])
-    tr(ct[:], cb[:, 0:128], ["cb0", "cb1", "cb2", "cb3", "cb4"], ["ct"])
-    q, rr, kk, fin = ct[:, 0:1], ct[:, 32:33], ct[:, 64:65], ct[:, 96:97]
+    for h in range(2):
+        for c in range(3):
+            cp("s", T.kb[:, 32 * c + 16 * h:32 * c + 16 * h + 16], cb[:, 96 + 48 * h + 16 * c:112 + 48 * h + 16 * c],
+               ["cb%d" % (3 + h)], ["kb%d%d" % (h, c)])
+    q, rr, fin = ct[:, 0:1], ct[:, 32:33], ct[:, 64:65]
     row, k16 = cb[:, 32:64], cb[:, 0:32]
-    GB, G64, G32, GF, GQ = lc[:, 0:16], lc[:, 16:20], lc[:, 20:22], lc[:, 22:24], lc[:, 24:60]
+    GB, G64, G32, GF, GQ = lc[:, 0:12], lc[:, 16:20], lc[:, 20:22], lc[:, 22:24], lc[:, 24:60]
     KW, LS, L1, L2, HD, TL = lr[:, 0:32], lr[:, 32:64], lr[:, 64:96], lr[:, 96:132], lr[:, 132:136], lr[:, 136:140]
-    ts(GB, cb[:, 32:48], 32.0, ALU.mult, ["ct"], ["GB"], kk, ALU.add)
     ts(tb[:, 16:32], cb[:, 0:16], q, ALU.is_equal, ["ct", "tz"], ["tz1"])
     ts(tb[:, 48:64], cb[:, 0:16], q, ALU.is_equal, ["ct", "tz"], ["tz2"], 2048.0, ALU.mult)
     ts(tb[:, 144:176], k16, q, ALU.is_lt, ["ct"], ["tl1"], 2048.0, ALU.add)
@@ -233,29 +244,38 @@ def rank_program(g, core, T, topo):
     ts(sc[:, 1:2], q, 15.0, ALU.is_equal, ["ct"], ["sc1"], 1024.0, ALU.mult)
     ts(sc[:, 2:3], q, 1.0, ALU.add, ["ct"], ["sc2"], 1.0 / 16, ALU.mult)
     ts(sc[:, 3:4], q, 1.0, ALU.add, ["ct"], ["sc3"])
+    tr(T.kt[:], T.kb[:], ["kb%d%d" % (h, c) for h in range(2) for c in range(3)], ["kt"])
     ts(G32, cb[:, 32:34], 32.0, ALU.mult, ["ct"], ["G32"], rr, ALU.add)
     ts(GF, cb[:, 32:34], 8.0, ALU.mult, ["ct"], ["GF"], fin, ALU.add)
-    ts(G64, cb[:, 128:132], sc[:, 0:1], ALU.add, ["cb5", "sc0"], ["G64"])
+    ts(G64, cb[:, 192:196], sc[:, 0:1], ALU.add, ["cb5", "sc0"], ["G64"])
     ts(T.jw[:], row, sc[:, 2:3], ALU.add, ["sc2"], ["jw"], 1.0 / 64, ALU.mult)
     quant(T.uq[:], T.us[:], T.ut[:], ["ut"], ["u"])
+    for c in range(3):
+        ts(lc[:, c:12:3], cb[:, 32:36], 128.0, ALU.mult, ["kt"], ["GB%d" % c], T.kt[:, 32 * c:32 * c + 1], ALU.add)
     ts(GQ, cb[:, 0:36], 0.0, ALU.mult, ["ct"], ["GQ"], q, ALU.add)
     ts(tb[:, 208:224], cb[:, 0:16], q, ALU.is_equal, ["ct"], ["tm1"], -4096.0, ALU.mult)
     ts(tb[:, 224:240], cb[:, 0:16], sc[:, 3:4], ALU.is_equal, ["sc3"], ["tm2"], 1024.0, ALU.mult)
     op("v", lambda: V.tensor_tensor(tb[:, 240:256], tb[:, 208:224], tb[:, 224:240], ALU.add), ["tm1", "tm2"], ["tm"])
-    cp("s", T.dm[:], tb[:, 240:256].indirect(GQ), ["tm", "GQ"], ["dm"])
-    for t in range(R):
-        op("s", lambda: S.activation(T["mk%d" % t][:], T.dm[:], ACT.Identity, 0.5, 0.0), ["dm"], ["mk%d" % t])
 
-    def state(t, tile, h, rd):
-        quant(T["aq%d" % t][:, H * h:H * h + H], T["as%d" % t][:, H * h:H * h + H],
-              tile[:, 4 * H * h:4 * H * (h + 1)], rd, ["a%d_%d" % (t, h)])
+    def halves(t, src, rd):
+        op("s", lambda: S.activation(T["mk%d" % t][:], src, ACT.Identity, 0.5, 0.0), rd, ["mk%d" % t])
 
-    def signs(t, h):
-        mm(bank("pb", h, 0, H), T.uq[:], T.us[:], T["aq%d" % t][:, H * h:H * h + H], T["as%d" % t][:, H * h:H * h + H],
-           ["u", "a%d_%d" % (t, h)], ["@b%d" % h])
+    def state(t, tile, n, rd):
+        lo, hi = PART[n]
+        quant(T["aq%d" % t][:, lo:hi], T["as%d" % t][:, lo:hi], tile[:, 4 * lo:4 * hi], rd, ["a%d_%d" % (t, n)])
 
-    def minus(h):
-        ts(T.xp[:, 16 + H * h:16 + H * h + H], bank("pb", h, 0, H), 0.0, ALU.is_lt, ["@b%d" % h], ["xp%d" % h])
+    def product(name, n, t, lq_, ls_, rd):
+        lo, hi = PART[n]
+        mm(bank("p" + name, n, 0, hi - lo), lq_, ls_, T["aq%d" % t][:, lo:hi], T["as%d" % t][:, lo:hi],
+           [rd, "a%d_%d" % (t, n)], ["@%s%d" % (name, n)])
+
+    def minus(n):
+        lo, hi = PART[n]
+        out, src = T.xp[:, 16 + lo:16 + hi], bank("pb", n, 0, hi - lo)
+        if n < 2:
+            op("s", lambda: S.activation(out, src, ACT.Sign), ["@b%d" % n], ["xp%d" % n])
+        else:
+            ts(out, src, 0.0, ALU.is_lt, ["@b%d" % n], ["xp%d" % n], -1.0, ALU.mult)
 
     def plane(b):
         op("s", lambda: S.activation(T.pp[:, PW * b:PW * b + C], bank("pa", b, 0, C), ACT.Copy, scale=0.03125),
@@ -267,38 +287,41 @@ def rank_program(g, core, T, topo):
             op("s", lambda: S.activation(T[tok][:, 513 * b:512 * b + 512:4], T.eye[:], ACT.Copy, scale=0.5 ** e),
                ["eye", tok], [tok + str(b)])
 
-    state(0, T.xt, 0, ["xt0"])
-    signs(0, 0)
-    minus(0)
-    state(0, T.xt, 1, ["xt1"])
+    halves(0, T.xt[:, 0:SL], ["xt0"])
+    for n in range(3):
+        state(0, T.xt, n, ["xt%d" % (n // 2)])
 
     for t in range(R):
         aq, ap = T["aq%d" % t], T["as%d" % t]
-        a0, a1 = "a%d_0" % t, "a%d_1" % t
         fl, mk, flt, mkt = T["fl%d" % t], T["mk%d" % t], "fl%d" % t, "mk%d" % t
         lq, lp = T["lq%d" % t], T["lp%d" % t]
-        for h in range(0 if t else 1, 2):
-            signs(t, h)
+        for n in range(3):
+            product("b", n, t, T.uq[:], T.us[:], "u")
         for b in range(4):
             mm(bank("pa", b, 0, C), T.wq[:, 128 * b:128 * b + 128], T.wp[:, 128 * b:128 * b + 128], aq[:], ap[:],
-               ["w", a0, a1], ["@a%d" % b])
+               ["w"] + ["a%d_%d" % (t, n) for n in range(3)], ["@a%d" % b])
+        minus(0)
+        minus(1)
         if t:
-            minus(0)
             plane(0)
+        else:
+            cp("s", T.dm[:], tb[:, 240:256].indirect(GQ), ["tm", "GQ"], ["dm"])
         tr(T.tt[:, 0:H], T.xp[:, 16:16 + H], ["xp0"], ["t0"])
         tr(T.tt[:, C:C + H], T.xp[:, 0:H], ["xp0", "xpa"], ["t1"])
-        minus(1)
-        tr(T.tt[:, H:C], T.xp[:, 16 + H:16 + C], ["xp1"], ["t2"])
-        tr(T.tt[:, C + H:1056], T.xp[:, H:544], ["xp0", "xp1", "xpb"], ["t3"])
-        cp("v", T.bg[:], T.tt[:, 0:1056].indirect(GB), ["t0", "t1", "t2", "t3", "GB"], ["bg"])
-        scan(T.kh[:], T.h8[:], T.bg[:], 0.0, ALU.mult, ALU.add, ["bg", "h8_0", "h8_1", "h8_2"], ["kh"])
-        cp("v", KW, T.kh[:, 7:256:8], ["kh"], ["KW"])
+        minus(2)
+        tr(T.tt[:, C + H:C + H + 128], T.xp[:, H:H + 128], ["xp0", "xp1"], ["t3"])
+        tr(T.tt[:, H:C], T.xp[:, 16 + H:16 + C], ["xp1", "xp2"], ["t2"])
+        tr(T.tt[:, C + H + 128:1056], T.xp[:, H + 128:544], ["xp1", "xp2", "xpb"], ["t4"])
+        ts(T.bg[:], T.tt[:, 0:1056].indirect(GB), 0.0, ALU.is_lt,
+           ["t0", "t1", "t2", "t3", "t4", "GB0", "GB1", "GB2"], ["bg"])
+        scan(T.kh[:], T.h6[:], T.bg[:], 0.0, ALU.mult, ALU.add, ["bg", "h6"], ["kh"])
+        cp("v", KW, T.kh[:, 5:192:6], ["kh"], ["KW"])
         op("s", lambda: S.activation(T.wl[:], tb[:, 144:208].indirect(KW), ACT.Copy, accum_out=T.acc[:, 0:1]),
            ["KW", "tl1", "tl2"], ["acc", "wl"])
         cp("v", T.wa[:, 1:C + 1], tb[:, 16:80].indirect(KW), ["KW", "tz", "tz1", "tz2"], ["wa"])
         cp("s", T.wb[:, 1:C + 1], tb[:, 0:64].indirect(KW), ["KW", "tz", "tz1", "tz2"], ["wb"])
         cp("s", T.wi[:, 0:16 * WS], tb[:, 80:144].indirect(lr[:, 0:WS]), ["KW", "ti1", "ti2"], ["wi"])
-        op("v", lambda: V.tensor_tensor(T.tmp[:], T.bg[:, 3:256:8], T.jw[:], ALU.add), ["bg", "jw"], ["tmp"])
+        op("v", lambda: V.tensor_tensor(T.tmp[:], T.bg[:, 1:192:6], T.jw[:], ALU.add), ["bg", "jw"], ["tmp"])
         scan(T.cum[:, 0:C + 1], T.wa[:, 0:C + 1], T.wa[:, 0:C + 1], T.acc[:, 0:1], ALU.add, ALU.max,
              ["wa", "wa0", "acc"], ["cumA"])
         ts(LS, T.tmp[:], 1024.0, ALU.mult, ["tmp"], ["LS"])
@@ -322,8 +345,7 @@ def rank_program(g, core, T, topo):
         cp("v", TL, T.y8[:, 1:8:2], ["y8a", "y8b"], ["TL"])
         cp("v", T.z32[:], T.yt[:].indirect(G32), ["yt", "G32"], ["z32"])
         tr(T.zt[:], T.z32[:], ["z32"], ["zt"])
-        cp("v", T.zi[:], T.zt[:].indirect(GF), ["zt", "GF"], ["zi"])
-        ts(T.za[:], T.zi[:], 2047, ALU.bitwise_and, ["zi"], ["za"])
+        ts(T.za[:], T.zt[:].indirect(GF), 2047, ALU.bitwise_and, ["zt", "GF"], ["za"])
         cp("v", L1, T.za[:], ["za"], ["L1"])
         cp("v", fl[:].indirect(L1), T.jf[:], ["L1", "jf"], [flt])
         scan(T.dg[:], T.dm[:], fl[:], 0.0, ALU.add, ALU.max, ["dm", flt], ["dg"])
@@ -347,8 +369,7 @@ def rank_program(g, core, T, topo):
                ["L1", "h%d" % b], ["ht%d_%d" % (b, h) for h in range(lo, hi)])
 
         def hand_on():
-            send(t, [(across[0], len(across), [r for r in second if r != rank], near_mask(rank),
-                      "f%d_%d" % (t, rank))], ["L%d_%d" % (t, slot(rank, i)) for i in across])
+            send(t, [(across[0], len(across), [r for r in second if r != rank], near_mask(rank), "f")], across)
 
         early = t > 0 and across == first[:1]
         if early:
@@ -365,11 +386,10 @@ def rank_program(g, core, T, topo):
             for b in range(4):
                 tail("sssv"[b], b)
             s0 = slot(rank, rank)
-            mine = "L%d_%d" % (t, s0)
             quant(lq[:, K * s0:K * s0 + 128], lp[:, K * s0:K * s0 + 128], T.et[:],
-                  ["e0", "e1", "e2", "e3", "epad"], [mine])
+                  ["e0", "e1", "e2", "e3", "epad"], ["L%d_%d" % (t, s0), "M%d_%d" % (t, s0)])
             for call in plan(rank):
-                send(t, [(rank, 1, to, m, "%s%d_%d" % (kind, t, rank)) for to, m, kind in call], [mine])
+                send(t, [(rank, 1, to, m, kind) for to, m, kind in call], [rank])
         if t == 0:
             iota(T.fl1[:], [[0, SL]], H, ["fl1"])
         if across and not early:
@@ -381,6 +401,7 @@ def rank_program(g, core, T, topo):
                     unit(e)
                 quant(T.iq[:, 512 * e:512 * e + 512], T.ip[:, 512 * e:512 * e + 512], T[tok][:],
                       [tok + str(b) for b in range(4)], ["i%d" % e])
+            halves(1, T.dm[:], ["dm"])
         if t == R - 1:
             quant(T.vq[:], T.vs[:], T.vt[:], ["vt"], ["v"])
 
@@ -404,7 +425,7 @@ def rank_program(g, core, T, topo):
                 have.append(i)
                 nm = "ba"[n % 2]
                 unpack(nm, rank - 1 - i, lq[:, K * lo:K * lo + 128], lp[:, K * lo:K * lo + 128],
-                       ["L%d_%d" % (t, lo), "L%d_%d" % (t, lo + 1)])
+                       ["%s%d_%d" % (a, t, j) for a in "LM" for j in (lo, lo + 1)])
                 o = K * (sl - lo)
                 for b in range(4):
                     src, out = bank("p" + nm, b, o, o + K), T.cc[:, b:256:4]
@@ -437,23 +458,24 @@ def rank_program(g, core, T, topo):
         else:
             for b in range(4 if t < R - 1 else 2):
                 back("sv"[b % 2], b)
-        for h in range(2):
-            if t == R - 1:
-                back("s", 2, h, h + 1)
-                back("v", 3, h, h + 1)
-            state(t + 1, T.ht, h, ["ht%d_%d" % (b, h) for b in range(4)])
+        for n in range(3):
+            if t == R - 1 and n < 2:
+                back("s", 2, n, n + 1)
+                back("v", 3, n, n + 1)
+            state(t + 1, T.ht, n, ["ht%d_%d" % (b, min(n, 1)) for b in range(4)])
 
     aq, ap = T["aq%d" % R], T["as%d" % R]
-    an = ["a%d_%d" % (R, h) for h in range(2)]
-    for h in range(2):
-        mm(bank("pa", h, 0, H), T.vq[:], T.vs[:], aq[:, H * h:H * h + H], ap[:, H * h:H * h + H], ["v", an[h]], ["@a%d" % h])
-        dma("y", T.oc[:, 4 * H * h:4 * H * (h + 1)], aq[:, H * h:H * h + H].bitcast(dt.uint8), [an[h]], [], "dout")
-    cp("s", T.ysb[:, 0:H], bank("pa", 0, 0, H), ["@a0"], ["y0"])
-    cp("v", T.ysb[:, H:C], bank("pa", 1, 0, H), ["@a1"], ["y1"])
-    dma("s", T.y[:, 0:H], T.ysb[:, 0:H], ["y0"], [], "dout2")
+    an = ["a%d_%d" % (R, n) for n in range(3)]
+    for n in range(3):
+        product("a", n, R, T.vq[:], T.vs[:], "v")
+        cp("ssv"[n], T.ysb[:, PART[n][0]:PART[n][1]], bank("pa", n, 0, PART[n][1] - PART[n][0]), ["@a%d" % n], ["y%d" % n])
+        if n == 0:
+            dma("s", T.y[:, 0:H], T.ysb[:, 0:H], ["y0"], [], "dout2")
+    dma("y", T.oc[:, 0:4 * H], aq[:, 0:H].bitcast(dt.uint8), an[:1], [], "dout")
+    dma("y", T.oc[:, 4 * H:4 * C], aq[:, H:C].bitcast(dt.uint8), an[1:], [], "dout")
+    dma("y", T.y[:, H:C], T.ysb[:, H:C], ["y1", "y2"], [], "dout")
     for k in range(4):
         dma("s", T.osc[4 * k:4 * k + 4, :], ap[32 * k:32 * k + 4, :], an, [], "dout2")
-    dma("y", T.y[:, H:C], T.ysb[:, H:C], ["y1"], [], "dout")
     for sem in ("cv", "cs", "ct", "cg", "dv", "dw", "dout", "dout2"):
         g.sync.wait_ge(T.sem[sem], count[sem])
     if "ls" in count:

@@ -7,6 +7,8 @@ SL = C + K
 PW = C + 16
 WS, GS = 22, 20
 PART = ((0, H), (H, H + 128), (H + 128, C))
+ZW, XW = 140, 130
+TINY = 1e-37
 F, B, I, U = "float32", "bfloat16", "int32", "uint16"
 Q4, U8 = "float8_e4m3fn_x4", "uint8"
 
@@ -21,18 +23,18 @@ SCRATCH = {
     "wq": _sb(512, Q4), "wp": _sb(512, U8), "iq": _sb(512 * (N - 1), Q4), "ip": _sb(512 * (N - 1), U8),
     "aq0": _sb(C, Q4), "as0": _sb(C, U8), "aq1": _sb(C, Q4), "as1": _sb(C, U8), "aq2": _sb(C, Q4), "as2": _sb(C, U8),
     "lq0": _sb(9 * K, Q4), "lp0": _sb(9 * K, U8), "lq1": _sb(9 * K, Q4), "lp1": _sb(9 * K, U8),
-    "cq": _sb(128, Q4), "cp": _sb(128, U8),
+    "cq": _sb(128, Q4), "cp": _sb(128, U8), "zq": _sb(ZW, Q4), "zp": _sb(ZW, U8),
+    "sq0": _sb(XW, Q4), "sp0": _sb(XW, U8), "sq1": _sb(XW, Q4), "sp1": _sb(XW, U8),
     "pa": ("psum", [128, 2048], F), "pb": ("psum", [128, 2048], F),
-    "cb": _sb(200, F), "ct": _sb(96, F), "kb": _sb(96, F), "kt": _sb(96, F),
-    "sc": _sb(8, F), "tb": _sb(256, F), "lc": _sb(64, U), "lr": _sb(144, U),
-    "ones": _sb(512, B), "eye": _sb(128, B), "id0": _sb(2048, B), "id1": _sb(2048, B),
-    "h6": _sb(192, B), "r16": _sb(512, B), "jf": _sb(C, B), "jw": _sb(32, F), "dm": _sb(SL, B),
-    "xp": _sb(544, B), "tt": _sb(1056, B), "bg": _sb(192, B), "kh": _sb(192, B), "tmp": _sb(32, F),
+    "cb": _sb(208, F), "ct": _sb(96, F), "sc": _sb(8, F), "tb": _sb(288, F), "lc": _sb(64, U), "lr": _sb(176, U),
+    "ones": _sb(128, B), "eye": _sb(128, B), "id0": _sb(2048, B), "id1": _sb(2048, B), "zt": _sb(4 * ZW, B),
+    "k16": _sb(512, B), "r16": _sb(512, B), "jf": _sb(C, B), "jw": _sb(32, F), "dm": _sb(SL, B),
+    "xs": _sb(C + 16, B), "tmp": _sb(32, F),
     "wa": _sb(520, F), "wb": _sb(520, F), "wl": _sb(C, F), "wi": _sb(C, F), "acc": _sb(8, F),
-    "cum": _sb(1544, F), "x4": _sb(4, I), "y8": _sb(8, I),
+    "cum": _sb(2 * C + 8, F), "x4": _sb(4, I), "y8": _sb(8, I),
     "vv": _sb(C, F), "vt2": _sb(C, F), "vs2": _sb(C, F),
-    "y64": _sb(64, F), "yt": _sb(64, F), "z32": _sb(32, I), "zt": _sb(32, I), "za": _sb(32, I),
-    "fl0": _sb(SL, B), "fl1": _sb(SL, B), "dg": _sb(SL, "float16"), "mk0": _sb(SL, B), "mk1": _sb(SL, B),
+    "y32": _sb(32, I), "yt": _sb(32, I), "za": _sb(32, I), "m64": _sb(64, I), "mt": _sb(64, I),
+    "fl": _sb(SL, B), "dg": _sb(SL, "float16"), "mk": _sb(SL, B),
     "pp": _sb(4 * PW, B), "ps": _sb(4 * SL, B), "hs": _sb(4 * SL, B), "et": _sb(512, B), "cc": _sb(512, B),
     "cs": _sb(4 * K, B), "ht": _sb(4 * C, B), "ysb": _sb(C, F),
 }
@@ -99,6 +101,12 @@ def rank_program(g, core, T, topo):
         else:
             op("v", lambda: V.tensor_scalar(out, in0, s1, s2, op0, op1), rd, wr)
 
+    def tt(out, in0, in1, op0, rd, wr):
+        op("v", lambda: V.tensor_tensor(out, in0, in1, op0), rd, wr)
+
+    def act(out, in_, fn, scale, bias, rd, wr):
+        op("s", lambda: S.activation(out, in_, fn, bias, scale), rd, wr)
+
     def cp(q, out, in_, rd, wr):
         if q == "v":
             op("v", lambda: V.tensor_copy(out, in_), rd, wr)
@@ -108,8 +116,8 @@ def rank_program(g, core, T, topo):
     def fill(ap, val, wr):
         op("v", lambda: V.memset(ap, val), [], wr)
 
-    def iota(ap, pat, base, wr):
-        op("g", lambda: g.iota(ap, pat, base, 0, allow_small_or_imprecise_dtypes=True), [], wr)
+    def iota(ap, pat, base, wr, cm=0):
+        op("g", lambda: g.iota(ap, pat, base, cm, allow_small_or_imprecise_dtypes=True), [], wr)
 
     def scan(out, d0, d1, init, op0, op1, rd, wr):
         op("v", lambda: V.tensor_tensor_scan(out, d0, d1, init, op0, op1), rd, wr)
@@ -120,11 +128,11 @@ def rank_program(g, core, T, topo):
     def quant(q, s, in_, rd, wr):
         op("v", lambda: V.quantize_mx(q, s, in_), rd, wr)
 
-    def mm(out, lq, ls, rq, rs, rd, wr):
-        op("t", lambda: PE.matmul_mx(out, lq, ls, rq, rs, True, True), rd, wr)
+    def mm(out, lq, ls, rq, rs, rd, wr, start=True, stop=True):
+        op("t", lambda: PE.matmul_mx(out, lq, ls, rq, rs, start, stop), rd, wr)
 
-    def bank(name, b, lo, hi):
-        return T[name][:, 512 * b + lo:512 * b + hi]
+    def bank(name, b, lo, hi, step=1):
+        return T[name][:, 512 * b + lo:512 * b + hi:step]
 
     chips = [topo.chip(c) for c in cores]
     first = [r for r in range(N) if chips[r] == chips[0]]
@@ -200,65 +208,56 @@ def rank_program(g, core, T, topo):
     dma("y", T.vt[:], T.v[:], [], ["vt"], "dv")
 
     cb, ct, sc, tb, lc, lr = T.cb, T.ct, T.sc, T.tb, T.lc, T.lr
-    iota(cb[:, 0:32], [[0, 2], [1, 16]], 0, ["cb0"])
-    iota(cb[:, 32:64], [[1, 32]], 0, ["cb1"])
-    iota(cb[:, 64:96], [[0, 2], [1, 8], [16, 2]], 0, ["cb2"])
-    iota(cb[:, 96:144], [[32, 4], [544, 2], [-1, 6]], 5, ["cb3"])
-    iota(cb[:, 144:192], [[32, 4], [-512, 2], [-1, 6]], 533, ["cb4"])
-    iota(cb[:, 192:196], [[16, 2], [0, 2]], 15, ["cb5"])
-    iota(T.cum[:, 513:1024], [[0, 511]], 0, ["gap"])
-    fill(T.ones[:], 1.0, ["ones"])
-    op("g", lambda: g.affine_select(T.r16[:], T.ones[:], [[0, 32], [1, 16]], ALU.not_equal, 0.0, 0, 0), ["ones"], ["r16"])
-    iota(T.jf[:], [[1, C]], -H, ["jf"])
-    iota(T.fl0[:], [[0, SL]], H, ["fl0"])
+    k16, k32 = cb[:, 0:16], cb[:, 0:32]
+    q, val, fin = ct[:, 0:1], ct[:, 32:33], ct[:, 64:65]
+    G32, GD, GF, GQ = lc[:, 0:2], lc[:, 2:6], lc[:, 6:8], lc[:, 8:44]
+    KW, LS, L1, L2, HD, TL, LP = (lr[:, 0:32], lr[:, 32:64], lr[:, 64:96], lr[:, 96:132], lr[:, 132:136],
+                                  lr[:, 136:140], lr[:, 140:172])
+    iota(k32, [[0, 2], [1, 16]], 0, ["cb0"])
+    iota(cb[:, 64:96], [[16, 2], [1, 8], [32, 2]], 0, ["cb2"])
+    iota(cb[:, 128:136], [[-16, 8]], 0, ["pm"], 1)
+    iota(cb[:, 96:128], [[1, 32]], 0, ["row"])
+    iota(cb[:, 136:140], [[16, 2], [0, 2]], 0, ["dup"])
+    iota(T.k16[:], [[0, 32], [1, 16]], 0, ["k16"])
+    iota(T.jf[:], [[1, 32], [32, 16]], -H, ["jf"])
+    iota(T.fl[:], [[0, SL]], H, ["fl"])
     if rank:
-        op("g", lambda: g.affine_select(T.eye[:], T.ones[:, 0:128], [[-1, 128]], ALU.is_equal, 0.0, 0, 1), ["ones"], ["eye"])
+        iota(T.ones[:], [[0, 128]], 1, ["ones"])
+        op("g", lambda: g.affine_select(T.eye[:], T.ones[:], [[-1, 128]], ALU.is_equal, 0.0, 0, 1), ["ones"], ["eye"])
         for i in range(min(rank, 2)):
             iota(T["id%d" % i][:], [[0, 2048]], 0, ["id%d" % i])
-    fill(T.h6[:], 2.0, ["h6"])
-    fill(T.xp[:, 0:16], 0.0, ["xpa"])
-    fill(T.xp[:, 528:544], 0.0, ["xpb"])
-    fill(tb[:, 0:80], 0.0, ["tz"])
-    fill(T.h6[:, 0:192:6], 0.0, ["h6"])
+    fill(T.zt[:], 0.0, ["z0"])
+    ts(cb[:, 144:176], k32, 6.0, ALU.is_lt, ["cb0"], ["d0"], 2.0, ALU.mult)
+    ts(cb[:, 176:208], k32, 0.0, ALU.is_equal, ["cb0"], ["d1"], -0.5, ALU.mult)
+    fill(T.xs[:, C:C + 16], 0.0, ["xpad"])
+    scan(cb[:, 32:64], cb[:, 144:176], cb[:, 176:208], 0.0, ALU.mult, ALU.add, ["d0", "d1"], ["cb1"])
     fill(T.pp[:, C:4 * PW:PW], 0.0, ["pz"])
-    fill(T.wb[:, 0:1], 2049.0, ["wb0"])
     tr(ct[:], cb[:, 0:96], ["cb0", "cb1", "cb2"], ["ct"])
     fill(T.et[:, 256:512], 0.0, ["epad"])
-    fill(T.cc[:, 256:512], 0.0, ["cpad"])
-    for h in range(2):
-        for c in range(3):
-            cp("s", T.kb[:, 32 * c + 16 * h:32 * c + 16 * h + 16], cb[:, 96 + 48 * h + 16 * c:112 + 48 * h + 16 * c],
-               ["cb%d" % (3 + h)], ["kb%d%d" % (h, c)])
-    q, rr, fin = ct[:, 0:1], ct[:, 32:33], ct[:, 64:65]
-    row, k16 = cb[:, 32:64], cb[:, 0:32]
-    GB, G64, G32, GF, GQ = lc[:, 0:12], lc[:, 16:20], lc[:, 20:22], lc[:, 22:24], lc[:, 24:60]
-    KW, LS, L1, L2, HD, TL = lr[:, 0:32], lr[:, 32:64], lr[:, 64:96], lr[:, 96:132], lr[:, 132:136], lr[:, 136:140]
-    ts(tb[:, 16:32], cb[:, 0:16], q, ALU.is_equal, ["ct", "tz"], ["tz1"])
-    ts(tb[:, 48:64], cb[:, 0:16], q, ALU.is_equal, ["ct", "tz"], ["tz2"], 2048.0, ALU.mult)
-    ts(tb[:, 144:176], k16, q, ALU.is_lt, ["ct"], ["tl1"], 2048.0, ALU.add)
-    ts(tb[:, 176:208], k16, q, ALU.is_lt, ["ct"], ["tl2"], 2048.0, ALU.mult)
-    ts(tb[:, 80:112], k16, q, ALU.is_equal, ["ct"], ["ti1"])
-    ts(tb[:, 112:144], k16, q, ALU.is_equal, ["ct"], ["ti2"], 1.0 / 2048, ALU.mult)
-    ts(T.wa[:, 0:1], q, 4098.0, ALU.mult, ["ct"], ["wa0"], 65536.0, ALU.add)
-    ts(sc[:, 0:1], q, 32.0, ALU.mult, ["ct"], ["sc0"])
-    ts(sc[:, 1:2], q, 15.0, ALU.is_equal, ["ct"], ["sc1"], 1024.0, ALU.mult)
-    ts(sc[:, 2:3], q, 1.0, ALU.add, ["ct"], ["sc2"], 1.0 / 16, ALU.mult)
-    ts(sc[:, 3:4], q, 1.0, ALU.add, ["ct"], ["sc3"])
-    tr(T.kt[:], T.kb[:], ["kb%d%d" % (h, c) for h in range(2) for c in range(3)], ["kt"])
-    ts(G32, cb[:, 32:34], 32.0, ALU.mult, ["ct"], ["G32"], rr, ALU.add)
-    ts(GF, cb[:, 32:34], 8.0, ALU.mult, ["ct"], ["GF"], fin, ALU.add)
-    ts(G64, cb[:, 192:196], sc[:, 0:1], ALU.add, ["cb5", "sc0"], ["G64"])
-    ts(T.jw[:], row, sc[:, 2:3], ALU.add, ["sc2"], ["jw"], 1.0 / 64, ALU.mult)
+    for e in range(4):
+        ts(T.zt[:, 48 + 5 * e:4 * ZW:64], cb[:, 128:136], q, ALU.is_equal, ["ct", "pm", "z0"], ["z%d" % (e + 1)], val, ALU.mult)
+    quant(T.zq[:], T.zp[:], T.zt[:], ["z1", "z2", "z3", "z4"], ["zq"])
     quant(T.uq[:], T.us[:], T.ut[:], ["ut"], ["u"])
-    for c in range(3):
-        ts(lc[:, c:12:3], cb[:, 32:36], 128.0, ALU.mult, ["kt"], ["GB%d" % c], T.kt[:, 32 * c:32 * c + 1], ALU.add)
-    ts(GQ, cb[:, 0:36], 0.0, ALU.mult, ["ct"], ["GQ"], q, ALU.add)
-    ts(tb[:, 208:224], cb[:, 0:16], q, ALU.is_equal, ["ct"], ["tm1"], -4096.0, ALU.mult)
-    ts(tb[:, 224:240], cb[:, 0:16], sc[:, 3:4], ALU.is_equal, ["sc3"], ["tm2"], 1024.0, ALU.mult)
-    op("v", lambda: V.tensor_tensor(tb[:, 240:256], tb[:, 208:224], tb[:, 224:240], ALU.add), ["tm1", "tm2"], ["tm"])
-
-    def halves(t, src, rd):
-        op("s", lambda: S.activation(T["mk%d" % t][:], src, ACT.Identity, 0.5, 0.0), rd, ["mk%d" % t])
+    act(sc[:, 0:1], q, ACT.Identity, -1.0, 0.0, ["ct"], ["sc0"])
+    act(sc[:, 1:2], q, ACT.Identity, 1.0, -0.5, ["ct"], ["sc1"])
+    act(tb[:, 240:256], k16, ACT.Abs, 1.0, sc[:, 0:1], ["sc0"], ["ab"])
+    act(tb[:, 256:272], k16, ACT.Sign, -1.0, sc[:, 1:2], ["sc1"], ["sg"])
+    act(tb[:, 0:32], k32, ACT.Identity, 0.0, 0.0, ["cb0"], ["tz0"])
+    act(tb[:, 64:96], k32, ACT.Identity, 0.0, 0.0, ["cb0"], ["tz1"])
+    for at, v in ((32, 1.0), (48, 2048.0), (96, 1.0), (112, 1.0 / 2048)):
+        act(tb[:, at:at + 16], tb[:, 240:256], ACT.Relu, -v, v, ["ab"], ["te%d" % at])
+    act(tb[:, 160:176], tb[:, 256:272], ACT.Identity, 0.5, 2048.5, ["sg"], ["tl0"])
+    act(tb[:, 176:192], tb[:, 256:272], ACT.Identity, 1024.0, 1024.0, ["sg"], ["tl1"])
+    act(T.wa[:, 0:1], q, ACT.Identity, 4098.0, 65536.0, ["ct"], ["wa0"])
+    act(T.wb[:, 0:1], q, ACT.Identity, 0.0, 2049.0, ["ct"], ["wb0"])
+    cp("s", tb[:, 192:224], tb[:, 160:192], ["tl0", "tl1"], ["tl2"])
+    cp("s", tb[:, 128:160], tb[:, 96:128], ["te96", "te112"], ["te128"])
+    act(sc[:, 2:3], q, ACT.Identity, 128.0, 160.0, ["ct"], ["sc2"])
+    act(sc[:, 3:4], q, ACT.Identity, 32.0, 15.0, ["ct"], ["sc3"])
+    act(sc[:, 4:5], q, ACT.Relu, 1024.0, -14336.0, ["ct"], ["sc4"])
+    act(T.jw[:], cb[:, 96:128], ACT.Identity, 2048.0, sc[:, 2:3], ["row", "sc2"], ["jw"])
+    act(tb[:, 272:288], tb[:, 31:47], ACT.Identity, 1024.0, 0.0, ["tz0", "te32"], ["tm2"])
+    steps, picks, starts = ["tz0", "tz1", "te32", "te48"], ["te96", "te112", "te128"], ["tl0", "tl1", "tl2"]
 
     def state(t, tile, n, rd):
         lo, hi = PART[n]
@@ -268,14 +267,6 @@ def rank_program(g, core, T, topo):
         lo, hi = PART[n]
         mm(bank("p" + name, n, 0, hi - lo), lq_, ls_, T["aq%d" % t][:, lo:hi], T["as%d" % t][:, lo:hi],
            [rd, "a%d_%d" % (t, n)], ["@%s%d" % (name, n)])
-
-    def minus(n):
-        lo, hi = PART[n]
-        out, src = T.xp[:, 16 + lo:16 + hi], bank("pb", n, 0, hi - lo)
-        if n < 2:
-            op("s", lambda: S.activation(out, src, ACT.Sign), ["@b%d" % n], ["xp%d" % n])
-        else:
-            ts(out, src, 0.0, ALU.is_lt, ["@b%d" % n], ["xp%d" % n], -1.0, ALU.mult)
 
     def plane(b):
         op("s", lambda: S.activation(T.pp[:, PW * b:PW * b + C], bank("pa", b, 0, C), ACT.Copy, scale=0.03125),
@@ -287,69 +278,81 @@ def rank_program(g, core, T, topo):
             op("s", lambda: S.activation(T[tok][:, 513 * b:512 * b + 512:4], T.eye[:], ACT.Copy, scale=0.5 ** e),
                ["eye", tok], [tok + str(b)])
 
-    halves(0, T.xt[:, 0:SL], ["xt0"])
+    def fields(at, half):
+        x, y, tok = T.x4[:, 2 * half:2 * half + 2], 4 * half, "xy%d" % half
+        return (lambda: cp("v", x, T.cum[:, at:at + 2], ["cumA", "cumB"], [tok]),
+                lambda: ts(T.y8[:, y:y + 4:2], x, 2047, ALU.bitwise_and, [tok], [tok + "a"]),
+                lambda: ts(T.y8[:, y + 1:y + 4:2], x, 11, ALU.logical_shift_right, [tok], [tok + "b"]),
+                lambda: cp("v", TL if half else HD, T.y8[:, y:y + 4], [tok + "a", tok + "b"], ["TL" if half else "HD"]))
+
     for n in range(3):
         state(0, T.xt, n, ["xt%d" % (n // 2)])
 
     for t in range(R):
         aq, ap = T["aq%d" % t], T["as%d" % t]
-        fl, mk, flt, mkt = T["fl%d" % t], T["mk%d" % t], "fl%d" % t, "mk%d" % t
         lq, lp = T["lq%d" % t], T["lp%d" % t]
-        for n in range(3):
-            product("b", n, t, T.uq[:], T.us[:], "u")
-        for b in range(4):
+
+        def layer(b):
             mm(bank("pa", b, 0, C), T.wq[:, 128 * b:128 * b + 128], T.wp[:, 128 * b:128 * b + 128], aq[:], ap[:],
                ["w"] + ["a%d_%d" % (t, n) for n in range(3)], ["@a%d" % b])
-        minus(0)
-        minus(1)
+        for n in range(3):
+            product("b", n, t, T.uq[:], T.us[:], "u")
+            lo, hi = PART[n]
+            act(T.xs[:, lo:hi], bank("pb", n, 0, hi - lo), ACT.Sign, 1.0, TINY, ["@b%d" % n], ["xs%d" % n])
         if t:
+            layer(0)
             plane(0)
         else:
-            cp("s", T.dm[:], tb[:, 240:256].indirect(GQ), ["tm", "GQ"], ["dm"])
-        tr(T.tt[:, 0:H], T.xp[:, 16:16 + H], ["xp0"], ["t0"])
-        tr(T.tt[:, C:C + H], T.xp[:, 0:H], ["xp0", "xpa"], ["t1"])
-        minus(2)
-        tr(T.tt[:, C + H:C + H + 128], T.xp[:, H:H + 128], ["xp0", "xp1"], ["t3"])
-        tr(T.tt[:, H:C], T.xp[:, 16 + H:16 + C], ["xp1", "xp2"], ["t2"])
-        tr(T.tt[:, C + H + 128:1056], T.xp[:, H + 128:544], ["xp1", "xp2", "xpb"], ["t4"])
-        ts(T.bg[:], T.tt[:, 0:1056].indirect(GB), 0.0, ALU.is_lt,
-           ["t0", "t1", "t2", "t3", "t4", "GB0", "GB1", "GB2"], ["bg"])
-        scan(T.kh[:], T.h6[:], T.bg[:], 0.0, ALU.mult, ALU.add, ["bg", "h6"], ["kh"])
-        cp("v", KW, T.kh[:, 5:192:6], ["kh"], ["KW"])
-        op("s", lambda: S.activation(T.wl[:], tb[:, 144:208].indirect(KW), ACT.Copy, accum_out=T.acc[:, 0:1]),
-           ["KW", "tl1", "tl2"], ["acc", "wl"])
-        cp("v", T.wa[:, 1:C + 1], tb[:, 16:80].indirect(KW), ["KW", "tz", "tz1", "tz2"], ["wa"])
-        cp("s", T.wb[:, 1:C + 1], tb[:, 0:64].indirect(KW), ["KW", "tz", "tz1", "tz2"], ["wb"])
-        cp("s", T.wi[:, 0:16 * WS], tb[:, 80:144].indirect(lr[:, 0:WS]), ["KW", "ti1", "ti2"], ["wi"])
-        op("v", lambda: V.tensor_tensor(T.tmp[:], T.bg[:, 1:192:6], T.jw[:], ALU.add), ["bg", "jw"], ["tmp"])
-        scan(T.cum[:, 0:C + 1], T.wa[:, 0:C + 1], T.wa[:, 0:C + 1], T.acc[:, 0:1], ALU.add, ALU.max,
+            ts(T.r16[:], T.k16[:], 0.0, ALU.is_gt, ["k16"], ["r16"])
+            ts(GQ, T.k16[:, 0:36], 0.0, ALU.mult, ["k16", "ct"], ["GQ"], q, ALU.add)
+        for h in range(2):
+            quant(T["sq%d" % h][:], T["sp%d" % h][:], T.xs[:, 4 * h:4 * h + 4 * XW], ["xs0", "xs1", "xs2", "xpad"], ["sq%d" % h])
+        for n, s in enumerate((0, 2, 1, 3)):
+            o, z = s & 2, 12 - 4 * s
+            mm(bank("pb", 3, 0, 128), T.zq[:, z:z + 128], T.zp[:, z:z + 128],
+               T["sq%d" % (s & 1)][:, o:o + 128], T["sp%d" % (s & 1)][:, o:o + 128],
+               ["zq", "sq%d" % (s & 1)], ["@b3"] if n in (0, 3) else [], n == 0, n == 3)
+        for b in range(1 if t else 0, 4):
+            layer(b)
+        if t == 0:
+            tt(tb[:, 224:240], tb[:, 272:288], tb[:, 48:64], ALU.subtract, ["tm2", "te48"], ["tm"])
+            ts(G32, cb[:, 136:140:2], sc[:, 3:4], ALU.add, ["dup", "sc3"], ["G32"])
+        keys = bank("pb", 3, 0, 128, 4)
+        ts(KW, keys, 31.5, ALU.add, ["@b3"], ["KW"])
+        tt(T.tmp[:], keys, T.jw[:], ALU.add, ["@b3", "jw"], ["tmp"])
+        op("s", lambda: S.activation(T.wl[:], tb[:, 160:224].indirect(KW), ACT.Copy, accum_out=T.acc[:, 0:1]),
+           ["KW"] + starts, ["acc", "wl"])
+        cp("v", T.wa[:, 1:C + 1], tb[:, 32:96].indirect(KW), ["KW"] + steps, ["wa"])
+        cp("s", T.wb[:, 1:C + 1], tb[:, 0:64].indirect(KW), ["KW"] + steps, ["wb"])
+        cp("s", T.wi[:, 0:16 * WS], tb[:, 96:160].indirect(lr[:, 0:WS]), ["KW"] + picks, ["wi"])
+        ts(LS, T.tmp[:], 1.0 / 64, ALU.mult, ["tmp"], ["LS"])
+        scan(T.cum[:, 0:2 * C + 2:2], T.wa[:, 0:C + 1], T.wa[:, 0:C + 1], T.acc[:, 0:1], ALU.add, ALU.max,
              ["wa", "wa0", "acc"], ["cumA"])
-        ts(LS, T.tmp[:], 1024.0, ALU.mult, ["tmp"], ["LS"])
-        cp("v", T.wi[:, 16 * WS:C], tb[:, 80:144].indirect(lr[:, WS:32]), ["KW", "ti1", "ti2"], ["wi2"])
-        scan(T.cum[:, 1024:1024 + C + 1], T.wb[:, 0:C + 1], T.wb[:, 0:C + 1], T.cum[:, C:C + 1], ALU.add, ALU.max,
+        cp("v", T.wi[:, 16 * WS:C], tb[:, 96:160].indirect(lr[:, WS:32]), ["KW"] + picks, ["wi2"])
+        scan(T.cum[:, 1:2 * C + 2:2], T.wb[:, 0:C + 1], T.wb[:, 0:C + 1], T.cum[:, 2 * C:2 * C + 1], ALU.add, ALU.max,
              ["wb", "wb0", "cumA"], ["cumB"])
         for b in range(1 if t else 0, 4):
             plane(b)
-        if t == 0 and rank:
-            unit(0)
-        op("v", lambda: V.tensor_tensor(T.vv[:], T.cum[:, 0:1537].indirect(LS), T.wi[:], ALU.mult),
-           ["cumA", "cumB", "gap", "LS", "wi", "wi2"], ["vv"])
-        cp("v", T.x4[:], T.cum[:, 0:1537:512], ["cumA", "cumB"], ["x4"])
+        if t == 0:
+            cp("s", T.dm[:], tb[:, 224:240].indirect(GQ), ["tm", "GQ"], ["dm"])
+            if rank:
+                unit(0)
+        tails = fields(2 * C, 1) if not last else (lambda: None,) * 4
+        tt(T.vv[:], T.cum[:, 0:2 * C + 2].indirect(LS), T.wi[:], ALU.mult, ["cumA", "cumB", "LS", "wi", "wi2"], ["vv"])
+        tails[0]()
         tr(T.vt2[:], T.vv[:], ["vv"], ["vt2"])
-        ts(T.y8[:, 0:4], T.x4[:], 2047, ALU.bitwise_and, ["x4"], ["y8a"])
+        tails[1]()
         scan(T.vs2[:], T.r16[:], T.vt2[:], 0.0, ALU.mult, ALU.add, ["vt2", "r16"], ["vs2"])
-        ts(T.y8[:, 4:8], T.x4[:], 11, ALU.logical_shift_right, ["x4"], ["y8b"])
-        cp("v", T.y64[:], T.vs2[:].indirect(G64), ["vs2", "G64"], ["y64"])
-        cp("v", HD, T.y8[:, 0:8:2], ["y8a", "y8b"], ["HD"])
-        tr(T.yt[:], T.y64[:], ["y64"], ["yt"])
-        cp("v", TL, T.y8[:, 1:8:2], ["y8a", "y8b"], ["TL"])
-        cp("v", T.z32[:], T.yt[:].indirect(G32), ["yt", "G32"], ["z32"])
-        tr(T.zt[:], T.z32[:], ["z32"], ["zt"])
-        ts(T.za[:], T.zt[:].indirect(GF), 2047, ALU.bitwise_and, ["zt", "GF"], ["za"])
-        cp("v", L1, T.za[:], ["za"], ["L1"])
-        cp("v", fl[:].indirect(L1), T.jf[:], ["L1", "jf"], [flt])
-        scan(T.dg[:], T.dm[:], fl[:], 0.0, ALU.add, ALU.max, ["dm", flt], ["dg"])
-        ts(L2, T.dg[:, 15:SL:16], sc[:, 1:2], ALU.add, ["dg", "sc1"], ["L2"], float(H - 1024), ALU.add)
+        tails[2]()
+        cp("v", T.y32[:], T.vs2[:].indirect(G32), ["vs2", "G32"], ["y32"])
+        tails[3]()
+        tr(T.yt[:], T.y32[:], ["y32"], ["yt"])
+        ts(T.za[:], T.yt[:], 2047, ALU.bitwise_and, ["yt"], ["za"])
+        cp("v", LP, T.za[:], ["za"], ["LP"])
+        cp("v", T.fl[:].indirect(LP), T.jf[:], ["LP", "jf"], ["fl"])
+        scan(T.dg[:], T.dm[:], T.fl[:], 0.0, ALU.add, ALU.max, ["dm", "fl"], ["dg"])
+        ts(L2, T.dg[:, 15:SL:16], sc[:, 4:5], ALU.add, ["dg", "sc4"], ["L2"], float(H - 1024), ALU.add)
+        ts(T.mk[:], T.fl[:], float(H), ALU.is_lt, ["fl"], ["mk"], 0.5, ALU.mult)
 
         def srt(q_, b, lo=0, hi=SL // 16, part=""):
             cp(q_, T.ps[:, SL * b + 16 * lo:SL * b + 16 * hi],
@@ -357,15 +360,14 @@ def rank_program(g, core, T, topo):
                ["L2", "pz", "p%d" % b], ["s%d%s" % (b, part)])
 
         def run(b):
-            scan(T.hs[:, SL * b:SL * b + SL], mk[:], T.ps[:, SL * b:SL * b + SL], 0.0, ALU.mult, ALU.max,
-                 [mkt, "s%d" % b, "s%dx" % b], ["h%d" % b])
+            scan(T.hs[:, SL * b:SL * b + SL], T.mk[:], T.ps[:, SL * b:SL * b + SL], 0.0, ALU.mult, ALU.max,
+                 ["mk", "s%d" % b, "s%dx" % b], ["h%d" % b])
 
         def tail(q_, b):
             cp(q_, T.et[:, b:256:4], T.hs[:, SL * b:SL * b + SL].indirect(TL), ["TL", "h%d" % b], ["e%d" % b])
 
-        def back(q_, b, lo=0, hi=2):
-            cp(q_, T.ht[:, 4 * H * lo + b:4 * H * hi:4],
-               T.hs[:, SL * b:SL * b + SL].indirect(lr[:, 64 + 16 * lo:64 + 16 * hi]),
+        def back(q_, b, lo=0, hi=4):
+            cp(q_, T.ht[:, C * lo + b:C * hi:4], T.hs[:, SL * b:SL * b + SL].indirect(lr[:, 64 + 8 * lo:64 + 8 * hi]),
                ["L1", "h%d" % b], ["ht%d_%d" % (b, h) for h in range(lo, hi)])
 
         def hand_on():
@@ -378,7 +380,6 @@ def rank_program(g, core, T, topo):
         srt("s", 2)
         srt("s", 3, 0, GS)
         srt("v", 0)
-        cp("v", mk[:].indirect(HD), T.et[:, 256:256 + K], ["HD", "epad"], [mkt])
         srt("v", 3, GS, SL // 16, "x")
         if not last:
             for b in range(4):
@@ -390,19 +391,31 @@ def rank_program(g, core, T, topo):
                   ["e0", "e1", "e2", "e3", "epad"], ["L%d_%d" % (t, s0), "M%d_%d" % (t, s0)])
             for call in plan(rank):
                 send(t, [(rank, 1, to, m, kind) for to, m, kind in call], [rank])
-        if t == 0:
-            iota(T.fl1[:], [[0, SL]], H, ["fl1"])
         if across and not early:
             hand_on()
         if t == 0:
+            ts(GD, cb[:, 136:140], q, ALU.add, ["dup", "ct"], ["GD"])
+            ts(GF, cb[:, 96:98], 8.0, ALU.mult, ["row", "ct"], ["GF"], fin, ALU.add)
+        heads = fields(0, 0) if rank else (lambda: None,) * 4
+        heads[0]()
+        cp("v", T.m64[:], T.za[:].indirect(GD), ["za", "GD"], ["m64"])
+        heads[1]()
+        tr(T.mt[:], T.m64[:], ["m64"], ["mt"])
+        heads[2]()
+        cp("v", L1, T.mt[:].indirect(GF), ["mt", "GF"], ["L1"])
+        heads[3]()
+        if t == 0:
+            if rank:
+                fill(T.cc[:, 256:512], 0.0, ["cpad"])
             for e in range(rank):
                 tok = "id%d" % (e % 2)
                 if e:
                     unit(e)
                 quant(T.iq[:, 512 * e:512 * e + 512], T.ip[:, 512 * e:512 * e + 512], T[tok][:],
                       [tok + str(b) for b in range(4)], ["i%d" % e])
-            halves(1, T.dm[:], ["dm"])
-        if t == R - 1:
+        if t < R - 1:
+            fill(T.fl[:], float(H), ["fl"])
+        else:
             quant(T.vq[:], T.vs[:], T.vt[:], ["vt"], ["v"])
 
         def unpack(nm, e, cq_, cp_, rd):
@@ -432,7 +445,7 @@ def rank_program(g, core, T, topo):
                     if n == 0:
                         cp("v", out, src, ["@%s%d" % (nm, b)], [cct[b]])
                     else:
-                        op("v", lambda: V.tensor_tensor(out, src, out, ALU.max), ["@%s%d" % (nm, b), cct[b]], [cct[b]])
+                        tt(out, src, out, ALU.max, ["@%s%d" % (nm, b), cct[b]], [cct[b]])
             quant(T.cq[:], T.cp[:], T.cc[:], cct + ["cpad"], ["cq"])
             nm = "ba"[len(seq) % 2]
             unpack(nm, 0, T.cq[:], T.cp[:], ["cq"])
@@ -452,17 +465,16 @@ def rank_program(g, core, T, topo):
             run(3)
             back("s", 0)
             back("s", 1)
-            if t < R - 1:
-                back("s", 2)
-                back("v", 3)
         else:
-            for b in range(4 if t < R - 1 else 2):
-                back("sv"[b % 2], b)
-        for n in range(3):
-            if t == R - 1 and n < 2:
-                back("s", 2, n, n + 1)
-                back("v", 3, n, n + 1)
-            state(t + 1, T.ht, n, ["ht%d_%d" % (b, min(n, 1)) for b in range(4)])
+            for b in range(2):
+                back("sv"[b], b)
+        back("s", 2, 0, 2)
+        back("s", 2, 2, 4)
+        back("s", 3, 3, 4)
+        for n, (lo, hi) in enumerate(((0, 2), (2, 3), (3, 4))):
+            if n < 2:
+                back("v", 3, lo, hi)
+            state(t + 1, T.ht, n, ["ht%d_%d" % (b, h) for b in range(4) for h in range(lo, hi)])
 
     aq, ap = T["aq%d" % R], T["as%d" % R]
     an = ["a%d_%d" % (R, n) for n in range(3)]
@@ -473,9 +485,9 @@ def rank_program(g, core, T, topo):
             dma("s", T.y[:, 0:H], T.ysb[:, 0:H], ["y0"], [], "dout2")
     dma("y", T.oc[:, 0:4 * H], aq[:, 0:H].bitcast(dt.uint8), an[:1], [], "dout")
     dma("y", T.oc[:, 4 * H:4 * C], aq[:, H:C].bitcast(dt.uint8), an[1:], [], "dout")
-    dma("y", T.y[:, H:C], T.ysb[:, H:C], ["y1", "y2"], [], "dout")
     for k in range(4):
-        dma("s", T.osc[4 * k:4 * k + 4, :], ap[32 * k:32 * k + 4, :], an, [], "dout2")
+        dma("y" if k < 3 else "s", T.osc[4 * k:4 * k + 4, :], ap[32 * k:32 * k + 4, :], an, [], "dout" if k < 3 else "dout2")
+    dma("s", T.y[:, H:C], T.ysb[:, H:C], ["y1", "y2"], [], "dout2")
     for sem in ("cv", "cs", "ct", "cg", "dv", "dw", "dout", "dout2"):
         g.sync.wait_ge(T.sem[sem], count[sem])
     if "ls" in count:

@@ -5,10 +5,12 @@ N, C, K, R = 8, 512, 64, 2
 H = C // 2
 SL = C + K
 PW = C + 16
-WS, GS = 22, 20
+WS, GS = 22, 12
 PART = ((0, H), (H, H + 128), (H + 128, C))
 ZW, XW = 140, 130
 TINY = 1e-37
+FAR = 1 << 18
+MANY = 5
 F, B, I, U = "float32", "bfloat16", "int32", "uint16"
 Q4, U8 = "float8_e4m3fn_x4", "uint8"
 
@@ -27,7 +29,7 @@ SCRATCH = {
     "sq0": _sb(XW, Q4), "sp0": _sb(XW, U8), "sq1": _sb(XW, Q4), "sp1": _sb(XW, U8),
     "pa": ("psum", [128, 2048], F), "pb": ("psum", [128, 2048], F),
     "cb": _sb(208, F), "ct": _sb(96, F), "sc": _sb(8, F), "tb": _sb(288, F), "lc": _sb(64, U), "lr": _sb(176, U),
-    "ones": _sb(128, B), "eye": _sb(128, B), "id0": _sb(2048, B), "id1": _sb(2048, B), "zt": _sb(4 * ZW, B),
+    "ones": _sb(PW, B), "ln": _sb(PW * (N - 1), B), "zt": _sb(4 * ZW, B),
     "k16": _sb(512, B), "r16": _sb(512, B), "jf": _sb(C, B), "jw": _sb(32, F), "dm": _sb(SL, B),
     "xs": _sb(C + 16, B), "tmp": _sb(32, F),
     "wa": _sb(520, F), "wb": _sb(520, F), "wl": _sb(C, F), "wi": _sb(C, F), "acc": _sb(8, F),
@@ -137,34 +139,45 @@ def rank_program(g, core, T, topo):
     chips = [topo.chip(c) for c in cores]
     first = [r for r in range(N) if chips[r] == chips[0]]
     second = [r for r in range(N) if chips[r] != chips[0]]
-    taker = {r: second[max(len(second) - 2 - i, 0)] for i, r in enumerate(first)}
+    taker = [dict(zip(first, (second[2], second[1], second[0], second[0]))),
+             dict(zip(first, (second[3], second[1], second[3], second[2])))]
 
-    def pieces(r):
+    def loads(t, r):
+        mine = [i for i in first if taker[t][i] == r]
+        return [[i] for i in mine] if t else [mine] if mine else []
+
+    def due(t, r):
+        own_chip = [i for i in range(r) if chips[i] == chips[r]]
         if r in first:
-            return [], [], list(range(r))
-        return ([i for i in first[1:] + first[:1] if taker[i] != r], [i for i in first if taker[i] == r],
-                [i for i in second if i < r])
+            return own_chip if t else own_chip[::-1]
+        mine = [i for i in first if taker[t][i] == r]
+        if t == 0:
+            return own_chip[::-1] + mine[::-1] + [i for i in (first[0], first[1], first[3], first[2]) if i not in mine]
+        rest = (first[1], first[3], second[0], first[2], second[1], second[2])
+        return first[:1] + [i for i in mine if i != first[0]] + [i for i in rest if i < r and i not in mine]
 
-    def slot(r, i):
-        a, b, c = pieces(r)
-        return (a + b + c + [r]).index(i)
+    def slot(t, r, i):
+        d = due(t, r)
+        return len(d) - ([r] + d).index(i)
 
     def bits(m):
         return bin(m).count("1")
 
     def far_mask(r):
-        return topo.mask(cores[r], cores[taker[r]])
+        return topo.mask(cores[r], cores[second[0]])
 
     def near_mask(r):
         other = [i for i in range(N) if chips[i] == chips[r] and i != r][0]
         m = topo.mask(cores[r], cores[other])
         return m & ~far_mask(r) if r in first else m
 
-    def plan(r):
+    def plan(t, r):
         to = [i for i in range(N - 1, r, -1) if chips[i] == chips[r]]
         if r not in first:
             return [[(to, near_mask(r), "o")]] if to else []
-        calls = [[([taker[r]], far_mask(r), "x")] + ([(to[:2], near_mask(r), "o")] if to else [])]
+        if t == 0 and len(to) > 2:
+            to = to[-1:] + to[:-1]
+        calls = [[([taker[t][r]], far_mask(r), "x")] + ([(to[:2], near_mask(r), "o")] if to else [])]
         return calls + ([[(to[2:], far_mask(r), "o")]] if to[2:] else [])
 
     def dst(r):
@@ -173,29 +186,29 @@ def rank_program(g, core, T, topo):
 
     def send(t, groups, have):
         for name, wide in (("lp%d" % t, False), ("lq%d" % t, True)):
-            order("g", ["%s%d_%d" % ("L" if wide else "M", t, slot(rank, i)) for i in have], [])
+            order("g", ["%s%d_%d" % ("L" if wide else "M", t, slot(t, rank, i)) for i in have], [])
 
             def view(r, i, n):
-                a = T[name][:, K * slot(r, i):K * (slot(r, i) + n)]
+                a = T[name][:, K * slot(t, r, i):K * (slot(t, r, i) + n)]
                 return a.bitcast(dt.uint8) if wide else a
             trs = [RemoteDMATransfer(dst_ids=[dst(r) for r in to], dma_engine_mask=m,
-                                     remote_sem=T.sem["%s%d_%d" % ("xs" if kind == "x" and not wide else kind, t, rank)],
+                                     remote_sem=T.sem["%s%d_%d" % ("xs" if kind == "x" and not wide else kind, t, i)],
                                      src=view(rank, i, n), dsts=[view(r, i, n) for r in to])
                    for i, n, to, m, kind in groups]
             g.remote_dma_fused(trs, local_sem=T.sem.ls)
             count["ls"] = count.get("ls", 0) + sum(bits(x[3]) for x in groups)
 
-    handed, across, near = pieces(rank)
     for t in range(R):
-        for i in handed + across + near:
-            if i in handed:
-                evs = [("f%d_%d" % (t, taker[i]), 2 * bits(near_mask(taker[i])), None, {})] * 2
+        for i in due(t, rank):
+            if chips[i] != chips[rank] and taker[t][i] != rank:
+                lead = [x[0] for x in loads(t, taker[t][i]) if i in x][0]
+                evs = [("f%d_%d" % (t, lead), 2 * bits(near_mask(taker[t][i])), None, {})] * 2
             else:
-                m, kind = [(m, kind) for call in plan(i) for to, m, kind in call if rank in to][0]
+                m, kind = [(m, kind) for call in plan(t, i) for to, m, kind in call if rank in to][0]
                 evs = [("o%d_%d" % (t, i), 2 * bits(m), None, {})] * 2
                 if kind == "x":
                     evs = [("x%d_%d" % (t, i), bits(m), None, {}), ("xs%d_%d" % (t, i), bits(m), None, {})]
-            writer["L%d_%d" % (t, slot(rank, i))], writer["M%d_%d" % (t, slot(rank, i))] = evs
+            writer["L%d_%d" % (t, slot(t, rank, i))], writer["M%d_%d" % (t, slot(t, rank, i))] = evs
     last = rank == N - 1
 
     cut = 4 * PART[2][0]
@@ -218,45 +231,39 @@ def rank_program(g, core, T, topo):
     iota(cb[:, 128:136], [[-16, 8]], 0, ["pm"], 1)
     iota(cb[:, 96:128], [[1, 32]], 0, ["row"])
     iota(cb[:, 136:140], [[16, 2], [0, 2]], 0, ["dup"])
+    if rank:
+        fill(T.ones[:], 1.0, ["ones"])
+        op("g", lambda: g.affine_select(T.ln[:, 0:PW], T.ones[:], [[-1, PW]], ALU.is_equal, 0.0, 3, 4), ["ones"], ["ln0"])
     iota(T.k16[:], [[0, 32], [1, 16]], 0, ["k16"])
     iota(T.jf[:], [[1, 32], [32, 16]], -H, ["jf"])
-    iota(T.fl[:], [[0, SL]], H, ["fl"])
-    if rank:
-        iota(T.ones[:], [[0, 128]], 1, ["ones"])
-        op("g", lambda: g.affine_select(T.eye[:], T.ones[:], [[-1, 128]], ALU.is_equal, 0.0, 0, 1), ["ones"], ["eye"])
-        for i in range(min(rank, 2)):
-            iota(T["id%d" % i][:], [[0, 2048]], 0, ["id%d" % i])
+    iota(T.fl[:], [[0, SL]], -FAR, ["fl"])
     fill(T.zt[:], 0.0, ["z0"])
     ts(cb[:, 144:176], k32, 6.0, ALU.is_lt, ["cb0"], ["d0"], 2.0, ALU.mult)
     ts(cb[:, 176:208], k32, 0.0, ALU.is_equal, ["cb0"], ["d1"], -0.5, ALU.mult)
     fill(T.xs[:, C:C + 16], 0.0, ["xpad"])
     scan(cb[:, 32:64], cb[:, 144:176], cb[:, 176:208], 0.0, ALU.mult, ALU.add, ["d0", "d1"], ["cb1"])
-    fill(T.pp[:, C:4 * PW:PW], 0.0, ["pz"])
+    fill(T.pp[:, 0:4 * PW:PW], 0.0, ["pz"])
     tr(ct[:], cb[:, 0:96], ["cb0", "cb1", "cb2"], ["ct"])
-    fill(T.et[:, 256:512], 0.0, ["epad"])
+    fill(T.et[:, 0 if last else 256:512], 0.0, ["epad"])
     for e in range(4):
         ts(T.zt[:, 48 + 5 * e:4 * ZW:64], cb[:, 128:136], q, ALU.is_equal, ["ct", "pm", "z0"], ["z%d" % (e + 1)], val, ALU.mult)
-    quant(T.zq[:], T.zp[:], T.zt[:], ["z1", "z2", "z3", "z4"], ["zq"])
-    quant(T.uq[:], T.us[:], T.ut[:], ["ut"], ["u"])
-    act(sc[:, 0:1], q, ACT.Identity, -1.0, 0.0, ["ct"], ["sc0"])
-    act(sc[:, 1:2], q, ACT.Identity, 1.0, -0.5, ["ct"], ["sc1"])
-    act(tb[:, 240:256], k16, ACT.Abs, 1.0, sc[:, 0:1], ["sc0"], ["ab"])
-    act(tb[:, 256:272], k16, ACT.Sign, -1.0, sc[:, 1:2], ["sc1"], ["sg"])
     act(tb[:, 0:32], k32, ACT.Identity, 0.0, 0.0, ["cb0"], ["tz0"])
     act(tb[:, 64:96], k32, ACT.Identity, 0.0, 0.0, ["cb0"], ["tz1"])
     for at, v in ((32, 1.0), (48, 2048.0), (96, 1.0), (112, 1.0 / 2048)):
-        act(tb[:, at:at + 16], tb[:, 240:256], ACT.Relu, -v, v, ["ab"], ["te%d" % at])
-    act(tb[:, 160:176], tb[:, 256:272], ACT.Identity, 0.5, 2048.5, ["sg"], ["tl0"])
-    act(tb[:, 176:192], tb[:, 256:272], ACT.Identity, 1024.0, 1024.0, ["sg"], ["tl1"])
+        ts(tb[:, at:at + 16], k16, q, ALU.is_equal, ["ct"], ["te%d" % at], v, ALU.mult)
+    quant(T.zq[:], T.zp[:], T.zt[:], ["z1", "z2", "z3", "z4"], ["zq"])
+    ts(tb[:, 160:176], k16, q, ALU.is_lt, ["ct"], ["tl0"], 2048.0, ALU.add)
+    ts(tb[:, 176:192], k16, q, ALU.is_lt, ["ct"], ["tl1"], 2048.0, ALU.mult)
+    quant(T.uq[:], T.us[:], T.ut[:], ["ut"], ["u"])
     act(T.wa[:, 0:1], q, ACT.Identity, 4098.0, 65536.0, ["ct"], ["wa0"])
     act(T.wb[:, 0:1], q, ACT.Identity, 0.0, 2049.0, ["ct"], ["wb0"])
-    cp("s", tb[:, 192:224], tb[:, 160:192], ["tl0", "tl1"], ["tl2"])
-    cp("s", tb[:, 128:160], tb[:, 96:128], ["te96", "te112"], ["te128"])
     act(sc[:, 2:3], q, ACT.Identity, 128.0, 160.0, ["ct"], ["sc2"])
     act(sc[:, 3:4], q, ACT.Identity, 32.0, 15.0, ["ct"], ["sc3"])
     act(sc[:, 4:5], q, ACT.Relu, 1024.0, -14336.0, ["ct"], ["sc4"])
     act(T.jw[:], cb[:, 96:128], ACT.Identity, 2048.0, sc[:, 2:3], ["row", "sc2"], ["jw"])
     act(tb[:, 272:288], tb[:, 31:47], ACT.Identity, 1024.0, 0.0, ["tz0", "te32"], ["tm2"])
+    cp("s", tb[:, 128:160], tb[:, 96:128], ["te96", "te112"], ["te128"])
+    cp("s", tb[:, 192:224], tb[:, 160:192], ["tl0", "tl1"], ["tl2"])
     steps, picks, starts = ["tz0", "tz1", "te32", "te48"], ["te96", "te112", "te128"], ["tl0", "tl1", "tl2"]
 
     def state(t, tile, n, rd):
@@ -269,14 +276,30 @@ def rank_program(g, core, T, topo):
            [rd, "a%d_%d" % (t, n)], ["@%s%d" % (name, n)])
 
     def plane(b):
-        op("s", lambda: S.activation(T.pp[:, PW * b:PW * b + C], bank("pa", b, 0, C), ACT.Copy, scale=0.03125),
+        op("s", lambda: S.activation(T.pp[:, PW * b + 1:PW * b + C + 1], bank("pa", b, 0, C), ACT.Copy, scale=0.03125),
            ["@a%d" % b], ["p%d" % b])
 
-    def unit(e):
-        for b in range(4):
-            tok = "id%d" % (e % 2)
-            op("s", lambda: S.activation(T[tok][:, 513 * b:512 * b + 512:4], T.eye[:], ACT.Copy, scale=0.5 ** e),
-               ["eye", tok], [tok + str(b)])
+    powers = [0] if rank else []
+    for i in due(0, rank):
+        if rank - 1 - i not in powers:
+            powers.append(rank - 1 - i)
+    lines, units = powers[1:], [(e, b) for e in powers for b in range(4)]
+
+    def line(n):
+        for e in lines[:n]:
+            op("s", lambda: S.activation(T.ln[:, PW * e:PW * e + PW], T.ln[:, 0:PW], ACT.Copy, scale=0.5 ** e),
+               ["ln0"], ["ln%d" % e])
+        del lines[:n]
+
+    def unit(n):
+        for e, b in units[:n]:
+            o, z = 512 * e + 128 * b, PW * e + 3 - b
+            quant(T.iq[:, o:o + 128], T.ip[:, o:o + 128], T.ln[:, z:z + 512], ["ln%d" % e], ["i%d_%d" % (e, b)])
+        del units[:n]
+
+    def gap(n):
+        if rank >= MANY:
+            unit(n)
 
     def fields(at, half):
         x, y, tok = T.x4[:, 2 * half:2 * half + 2], 4 * half, "xy%d" % half
@@ -302,9 +325,12 @@ def rank_program(g, core, T, topo):
         if t:
             layer(0)
             plane(0)
+            quant(T.vq[:], T.vs[:], T.vt[:], ["vt"], ["v"])
         else:
             ts(T.r16[:], T.k16[:], 0.0, ALU.is_gt, ["k16"], ["r16"])
             ts(GQ, T.k16[:, 0:36], 0.0, ALU.mult, ["k16", "ct"], ["GQ"], q, ALU.add)
+            line(1)
+            gap(4)
         for h in range(2):
             quant(T["sq%d" % h][:], T["sp%d" % h][:], T.xs[:, 4 * h:4 * h + 4 * XW], ["xs0", "xs1", "xs2", "xpad"], ["sq%d" % h])
         for n, s in enumerate((0, 2, 1, 3)):
@@ -317,6 +343,7 @@ def rank_program(g, core, T, topo):
         if t == 0:
             tt(tb[:, 224:240], tb[:, 272:288], tb[:, 48:64], ALU.subtract, ["tm2", "te48"], ["tm"])
             ts(G32, cb[:, 136:140:2], sc[:, 3:4], ALU.add, ["dup", "sc3"], ["G32"])
+            gap(2)
         keys = bank("pb", 3, 0, 128, 4)
         ts(KW, keys, 31.5, ALU.add, ["@b3"], ["KW"])
         tt(T.tmp[:], keys, T.jw[:], ALU.add, ["@b3", "jw"], ["tmp"])
@@ -335,24 +362,37 @@ def rank_program(g, core, T, topo):
             plane(b)
         if t == 0:
             cp("s", T.dm[:], tb[:, 224:240].indirect(GQ), ["tm", "GQ"], ["dm"])
-            if rank:
-                unit(0)
-        tails = fields(2 * C, 1) if not last else (lambda: None,) * 4
-        tt(T.vv[:], T.cum[:, 0:2 * C + 2].indirect(LS), T.wi[:], ALU.mult, ["cumA", "cumB", "LS", "wi", "wi2"], ["vv"])
+            line(N)
+        nothing = (lambda: None,) * 4
+        tails = nothing if last else fields(2 * C, 1)
+        heads = fields(0, 0) if rank else nothing
+        halves = ((0, H), (H, C))
+        for n, (lo, hi) in enumerate(halves):
+            tt(T.vv[:, lo:hi], T.cum[:, 0:2 * C + 2].indirect(lr[:, 32 + lo // 16:32 + hi // 16]), T.wi[:, lo:hi], ALU.mult,
+               ["cumA", "cumB", "LS", "wi", "wi2"], ["vv%d" % n])
+        for n, (lo, hi) in enumerate(halves):
+            tr(T.vt2[:, lo:hi], T.vv[:, lo:hi], ["vv%d" % n], ["vt%d" % n])
+        for n, (lo, hi) in enumerate(halves):
+            scan(T.vs2[:, lo:hi], T.r16[:, lo:hi], T.vt2[:, lo:hi], 0.0, ALU.mult, ALU.add, ["vt%d" % n, "r16"], ["vs%d" % n])
         tails[0]()
-        tr(T.vt2[:], T.vv[:], ["vv"], ["vt2"])
+        cp("v", T.y32[:], T.vs2[:].indirect(G32), ["vs0", "vs1", "G32"], ["y32"])
         tails[1]()
-        scan(T.vs2[:], T.r16[:], T.vt2[:], 0.0, ALU.mult, ALU.add, ["vt2", "r16"], ["vs2"])
-        tails[2]()
-        cp("v", T.y32[:], T.vs2[:].indirect(G32), ["vs2", "G32"], ["y32"])
-        tails[3]()
         tr(T.yt[:], T.y32[:], ["y32"], ["yt"])
+        tails[2]()
         ts(T.za[:], T.yt[:], 2047, ALU.bitwise_and, ["yt"], ["za"])
+        heads[0]()
         cp("v", LP, T.za[:], ["za"], ["LP"])
+        tails[3]()
+        gap(1)
         cp("v", T.fl[:].indirect(LP), T.jf[:], ["LP", "jf"], ["fl"])
+        heads[1]()
+        gap(1)
+        act(T.mk[:], T.fl[:], ACT.Relu, 0.5 / FAR, 0.5, ["fl"], ["mk"])
         scan(T.dg[:], T.dm[:], T.fl[:], 0.0, ALU.add, ALU.max, ["dm", "fl"], ["dg"])
-        ts(L2, T.dg[:, 15:SL:16], sc[:, 4:5], ALU.add, ["dg", "sc4"], ["L2"], float(H - 1024), ALU.add)
-        ts(T.mk[:], T.fl[:], float(H), ALU.is_lt, ["fl"], ["mk"], 0.5, ALU.mult)
+        heads[2]()
+        ts(L2, T.dg[:, 15:SL:16], sc[:, 4:5], ALU.add, ["dg", "sc4"], ["L2"], float(H + 1 - 1024), ALU.add)
+        heads[3]()
+        gap(1)
 
         def srt(q_, b, lo=0, hi=SL // 16, part=""):
             cp(q_, T.ps[:, SL * b + 16 * lo:SL * b + 16 * hi],
@@ -371,10 +411,11 @@ def rank_program(g, core, T, topo):
                ["L1", "h%d" % b], ["ht%d_%d" % (b, h) for h in range(lo, hi)])
 
         def hand_on():
-            send(t, [(across[0], len(across), [r for r in second if r != rank], near_mask(rank), "f")], across)
+            to = [r for r in second if r != rank]
+            for x in loads(t, rank):
+                send(t, [(x[0], len(x), to[::-1] if t else to, near_mask(rank), "f")], x)
 
-        early = t > 0 and across == first[:1]
-        if early:
+        if t:
             hand_on()
         srt("s", 1)
         srt("s", 2)
@@ -384,66 +425,50 @@ def rank_program(g, core, T, topo):
         if not last:
             for b in range(4):
                 run(b)
-            for b in range(4):
-                tail("sssv"[b], b)
-            s0 = slot(rank, rank)
-            quant(lq[:, K * s0:K * s0 + 128], lp[:, K * s0:K * s0 + 128], T.et[:],
-                  ["e0", "e1", "e2", "e3", "epad"], ["L%d_%d" % (t, s0), "M%d_%d" % (t, s0)])
-            for call in plan(rank):
-                send(t, [(rank, 1, to, m, kind) for to, m, kind in call], [rank])
-        if across and not early:
-            hand_on()
+            for b in range(3):
+                tail("s", b)
         if t == 0:
             ts(GD, cb[:, 136:140], q, ALU.add, ["dup", "ct"], ["GD"])
-            ts(GF, cb[:, 96:98], 8.0, ALU.mult, ["row", "ct"], ["GF"], fin, ALU.add)
-        heads = fields(0, 0) if rank else (lambda: None,) * 4
-        heads[0]()
-        cp("v", T.m64[:], T.za[:].indirect(GD), ["za", "GD"], ["m64"])
-        heads[1]()
-        tr(T.mt[:], T.m64[:], ["m64"], ["mt"])
-        heads[2]()
-        cp("v", L1, T.mt[:].indirect(GF), ["mt", "GF"], ["L1"])
-        heads[3]()
+        if not last:
+            tail("v", 3)
         if t == 0:
+            ts(GF, cb[:, 96:98], 8.0, ALU.mult, ["row", "ct"], ["GF"], fin, ALU.add)
+        s0 = slot(t, rank, rank)
+        quant(lq[:, K * s0:K * s0 + 128], lp[:, K * s0:K * s0 + 128], T.et[:],
+              ["e0", "e1", "e2", "e3", "epad"], ["L%d_%d" % (t, s0), "M%d_%d" % (t, s0)])
+        if not last:
+            for call in plan(t, rank):
+                send(t, [(rank, 1, to, m, kind) for to, m, kind in call], [rank])
+        if t == 0:
+            hand_on()
+        cp("v", T.m64[:], T.za[:].indirect(GD), ["za", "GD"], ["m64"])
+        unit(1)
+        tr(T.mt[:], T.m64[:], ["m64"], ["mt"])
+        if t == 0:
+            fill(T.fl[:], float(-FAR), ["fl"])
             if rank:
                 fill(T.cc[:, 256:512], 0.0, ["cpad"])
-            for e in range(rank):
-                tok = "id%d" % (e % 2)
-                if e:
-                    unit(e)
-                quant(T.iq[:, 512 * e:512 * e + 512], T.ip[:, 512 * e:512 * e + 512], T[tok][:],
-                      [tok + str(b) for b in range(4)], ["i%d" % e])
-        if t < R - 1:
-            fill(T.fl[:], float(H), ["fl"])
-        else:
-            quant(T.vq[:], T.vs[:], T.vt[:], ["vt"], ["v"])
+        cp("v", L1, T.mt[:].indirect(GF), ["mt", "GF"], ["L1"])
+        unit(4 * N)
 
         def unpack(nm, e, cq_, cp_, rd):
             for b in range(4):
                 o = 512 * e + 128 * b
                 mm(bank("p" + nm, b, 0, 128), T.iq[:, o:o + 128], T.ip[:, o:o + 128], cq_, cp_,
-                   ["i%d" % e] + rd, ["@%s%d" % (nm, b)])
+                   ["i%d_%d" % (e, b)] + rd, ["@%s%d" % (nm, b)])
 
         if rank:
-            soon = [i for i in handed if i == first[0]]
-            seq = (soon + across + near if t else near + across + soon) + [i for i in handed if i not in soon]
-            if rank in first:
-                seq = near[::-1]
+            seq = due(t, rank)
             cct = ["c%d" % b for b in range(4)]
-            have = [] if last else [rank]
             for n, i in enumerate(seq):
-                sl = slot(rank, i)
-                there = [slot(rank, j) for j in have]
-                lo = sl - 1 if (sl - 1 in there and sl + 1 not in there) else sl
-                have.append(i)
+                lo = slot(t, rank, i)
                 nm = "ba"[n % 2]
                 unpack(nm, rank - 1 - i, lq[:, K * lo:K * lo + 128], lp[:, K * lo:K * lo + 128],
                        ["%s%d_%d" % (a, t, j) for a in "LM" for j in (lo, lo + 1)])
-                o = K * (sl - lo)
                 for b in range(4):
-                    src, out = bank("p" + nm, b, o, o + K), T.cc[:, b:256:4]
+                    src, out = bank("p" + nm, b, 0, K), T.cc[:, b:256:4]
                     if n == 0:
-                        cp("v", out, src, ["@%s%d" % (nm, b)], [cct[b]])
+                        cp("s" if t else "v", out, src, ["@%s%d" % (nm, b)], [cct[b]])
                     else:
                         tt(out, src, out, ALU.max, ["@%s%d" % (nm, b), cct[b]], [cct[b]])
             quant(T.cq[:], T.cp[:], T.cc[:], cct + ["cpad"], ["cq"])

from concourse.bass import DstId, RemoteDMATransfer
from concourse.mybir import dt, AluOpType as ALU, ActivationFunctionType as ACT

N, C, K, R = 8, 512, 64, 2
H = C // 2
SL = C + K
PW = C + 16
WS, GS = 22, 12
PART = ((0, H), (H, H + 128), (H + 128, C))
ZW, XW = 140, 130
TINY = 1e-37
FAR = 1 << 18
MANY = 5
F, B, I, U = "float32", "bfloat16", "int32", "uint16"
Q4, U8 = "float8_e4m3fn_x4", "uint8"


def _sb(n, d):
    return ("sbuf", [128, n], d)


SCRATCH = {
    "xt": _sb(4 * C, B), "ut": _sb(512, B), "vt": _sb(512, B),
    "uq": _sb(128, Q4), "us": _sb(128, U8), "vq": _sb(128, Q4), "vs": _sb(128, U8),
    "wq": _sb(512, Q4), "wp": _sb(512, U8), "iq": _sb(512 * (N - 1), Q4), "ip": _sb(512 * (N - 1), U8),
    "aq0": _sb(C, Q4), "as0": _sb(C, U8), "aq1": _sb(C, Q4), "as1": _sb(C, U8), "aq2": _sb(C, Q4), "as2": _sb(C, U8),
    "lq0": _sb(9 * K, Q4), "lp0": _sb(9 * K, U8), "lq1": _sb(9 * K, Q4), "lp1": _sb(9 * K, U8),
    "cq": _sb(128, Q4), "cp": _sb(128, U8), "zq": _sb(ZW, Q4), "zp": _sb(ZW, U8),
    "sq0": _sb(XW, Q4), "sp0": _sb(XW, U8), "sq1": _sb(XW, Q4), "sp1": _sb(XW, U8),
    "pa": ("psum", [128, 2048], F), "pb": ("psum", [128, 2048], F),
    "cb": _sb(208, F), "ct": _sb(96, F), "sc": _sb(8, F), "tb": _sb(288, F), "lc": _sb(64, U), "lr": _sb(176, U),
    "ones": _sb(PW, B), "ln": _sb(PW * (N - 1), B), "zt": _sb(4 * ZW, B),
    "k16": _sb(512, B), "r16": _sb(512, B), "jf": _sb(C, B), "jw": _sb(32, F), "dm": _sb(SL, B),
    "xs": _sb(C + 16, B), "tmp": _sb(32, F),
    "wa": _sb(520, F), "wb": _sb(520, F), "wl": _sb(C, F), "wi": _sb(C, F), "acc": _sb(8, F),
    "cum": _sb(2 * C + 8, F), "x4": _sb(4, I), "y8": _sb(8, I),
    "vv": _sb(C, F), "vt2": _sb(C, F), "vs2": _sb(C, F),
    "y32": _sb(32, I), "yt": _sb(32, I), "za": _sb(32, I), "m64": _sb(64, I), "mt": _sb(64, I),
    "fl": _sb(SL, B), "dg": _sb(SL, "float16"), "mk": _sb(SL, B),
    "pp": _sb(4 * PW, B), "ps": _sb(4 * SL, B), "hs": _sb(4 * SL, B), "et": _sb(512, B), "cc": _sb(512, B),
    "cs": _sb(4 * K, B), "ht": _sb(4 * C, B), "ysb": _sb(C, F),
}
SEMAPHORES = (["cv", "cs", "ct", "cg", "ls", "dx0", "dx1", "du", "dv", "dw", "dout", "dout2"]
              + ["%s%d_%d" % (a, t, r) for a in ("x", "xs", "o", "f") for t in range(R) for r in range(N)])


def rank_program(g, core, T, topo):
    rank = T.rank_of(core)
    if rank is None:
        return
    cores = list(T.cores)
    eng = {"v": g.vector, "s": g.scalar, "t": g.tensor, "g": g, "y": g.sync}
    own = {"v": "cv", "s": "cs", "t": "ct", "g": "cg"}
    count = {}
    known = {q: {} for q in eng}
    writer, readers = {}, {}

    def need(q, ev):
        sem, n, _, kn = ev
        if known[q].get(sem, 0) < n:
            eng[q].wait_ge(T.sem[sem], n)
            known[q][sem] = n
        for s, m in kn.items():
            if known[q].get(s, 0) < m:
                known[q][s] = m

    def order(q, rd, wr):
        evs = []
        for t in rd:
            if t in writer:
                evs.append(writer[t])
            if t[0] == "@":
                evs += [e for e in readers.get(t, []) if e[2] != q]
        for t in wr:
            if t in writer:
                evs.append(writer[t])
            evs += readers.get(t, [])
        for e in sorted(evs, key=lambda e: -e[1]):
            need(q, e)

    def note(ev, rd, wr):
        for t in rd:
            readers.setdefault(t, []).append(ev)
        for t in wr:
            writer[t] = ev
            readers[t] = []

    def op(q, fn, rd, wr, sem=None, inc=1):
        order(q, rd, wr)
        sem = sem or own[q]
        fn().then_inc(T.sem[sem], inc)
        count[sem] = count.get(sem, 0) + inc
        note((sem, count[sem], q, dict(known[q])), rd, wr)

    def dma(q, out, in_, rd, wr, sem):
        op(q, lambda: eng[q].dma_start(out, in_), rd, wr, sem, 16)

    V, S, PE = g.vector, g.scalar, g.tensor

    def ts(out, in0, s1, op0, rd, wr, s2=None, op1=None):
        if op1 is None:
            op("v", lambda: V.tensor_scalar(out, in0, s1, None, op0), rd, wr)
        else:
            op("v", lambda: V.tensor_scalar(out, in0, s1, s2, op0, op1), rd, wr)

    def tt(out, in0, in1, op0, rd, wr):
        op("v", lambda: V.tensor_tensor(out, in0, in1, op0), rd, wr)

    def act(out, in_, fn, scale, bias, rd, wr):
        op("s", lambda: S.activation(out, in_, fn, bias, scale), rd, wr)

    def cp(q, out, in_, rd, wr):
        if q == "v":
            op("v", lambda: V.tensor_copy(out, in_), rd, wr)
        else:
            op("s", lambda: S.activation(out, in_, ACT.Copy), rd, wr)

    def fill(ap, val, wr):
        op("v", lambda: V.memset(ap, val), [], wr)

    def iota(ap, pat, base, wr, cm=0):
        op("g", lambda: g.iota(ap, pat, base, cm, allow_small_or_imprecise_dtypes=True), [], wr)

    def scan(out, d0, d1, init, op0, op1, rd, wr):
        op("v", lambda: V.tensor_tensor_scan(out, d0, d1, init, op0, op1), rd, wr)

    def tr(out, in_, rd, wr):
        op("v", lambda: V.transpose(out, in_), rd, wr)

    def quant(q, s, in_, rd, wr):
        op("v", lambda: V.quantize_mx(q, s, in_), rd, wr)

    def mm(out, lq, ls, rq, rs, rd, wr, start=True, stop=True):
        op("t", lambda: PE.matmul_mx(out, lq, ls, rq, rs, start, stop), rd, wr)

    def bank(name, b, lo, hi, step=1):
        return T[name][:, 512 * b + lo:512 * b + hi:step]

    chips = [topo.chip(c) for c in cores]
    first = [r for r in range(N) if chips[r] == chips[0]]
    second = [r for r in range(N) if chips[r] != chips[0]]
    taker = [dict(zip(first, (second[2], second[1], second[0], second[0]))),
             dict(zip(first, (second[3], second[1], second[3], second[2])))]

    def loads(t, r):
        mine = [i for i in first if taker[t][i] == r]
        return [[i] for i in mine] if t else [mine] if mine else []

    def due(t, r):
        own_chip = [i for i in range(r) if chips[i] == chips[r]]
        if r in first:
            return own_chip if t else own_chip[::-1]
        mine = [i for i in first if taker[t][i] == r]
        if t == 0:
            return own_chip[::-1] + mine[::-1] + [i for i in (first[0], first[1], first[3], first[2]) if i not in mine]
        rest = (first[1], first[3], second[0], first[2], second[1], second[2])
        return first[:1] + [i for i in mine if i != first[0]] + [i for i in rest if i < r and i not in mine]

    def slot(t, r, i):
        d = due(t, r)
        return len(d) - ([r] + d).index(i)

    def bits(m):
        return bin(m).count("1")

    def far_mask(r):
        return topo.mask(cores[r], cores[second[0]])

    def near_mask(r):
        other = [i for i in range(N) if chips[i] == chips[r] and i != r][0]
        m = topo.mask(cores[r], cores[other])
        return m & ~far_mask(r) if r in first else m

    def plan(t, r):
        to = [i for i in range(N - 1, r, -1) if chips[i] == chips[r]]
        if r not in first:
            return [[(to, near_mask(r), "o")]] if to else []
        if t == 0 and len(to) > 2:
            to = to[-1:] + to[:-1]
        calls = [[([taker[t][r]], far_mask(r), "x")] + ([(to[:2], near_mask(r), "o")] if to else [])]
        return calls + ([[(to[2:], far_mask(r), "o")]] if to[2:] else [])

    def dst(r):
        a = topo.addr(cores[r])
        return DstId(rid=a[0], pnc=a[1])

    def send(t, groups, have):
        for name, wide in (("lp%d" % t, False), ("lq%d" % t, True)):
            order("g", ["%s%d_%d" % ("L" if wide else "M", t, slot(t, rank, i)) for i in have], [])

            def view(r, i, n):
                a = T[name][:, K * slot(t, r, i):K * (slot(t, r, i) + n)]
                return a.bitcast(dt.uint8) if wide else a
            trs = [RemoteDMATransfer(dst_ids=[dst(r) for r in to], dma_engine_mask=m,
                                     remote_sem=T.sem["%s%d_%d" % ("xs" if kind == "x" and not wide else kind, t, i)],
                                     src=view(rank, i, n), dsts=[view(r, i, n) for r in to])
                   for i, n, to, m, kind in groups]
            g.remote_dma_fused(trs, local_sem=T.sem.ls)
            count["ls"] = count.get("ls", 0) + sum(bits(x[3]) for x in groups)

    for t in range(R):
        for i in due(t, rank):
            if chips[i] != chips[rank] and taker[t][i] != rank:
                lead = [x[0] for x in loads(t, taker[t][i]) if i in x][0]
                evs = [("f%d_%d" % (t, lead), 2 * bits(near_mask(taker[t][i])), None, {})] * 2
            else:
                m, kind = [(m, kind) for call in plan(t, i) for to, m, kind in call if rank in to][0]
                evs = [("o%d_%d" % (t, i), 2 * bits(m), None, {})] * 2
                if kind == "x":
                    evs = [("x%d_%d" % (t, i), bits(m), None, {}), ("xs%d_%d" % (t, i), bits(m), None, {})]
            writer["L%d_%d" % (t, slot(t, rank, i))], writer["M%d_%d" % (t, slot(t, rank, i))] = evs
    last = rank == N - 1

    cut = 4 * PART[2][0]
    dma("y", T.xt[:, 0:cut], T.x[:, 0:cut], [], ["xt0"], "dx0")
    dma("s", T.ut[:], T.u[:], [], ["ut"], "du")
    dma("y", T.xt[:, cut:4 * C], T.x[:, cut:4 * C], [], ["xt1"], "dx1")
    order("y", ["xt0", "xt1"], [])
    dma("y", T.wq[:].bitcast(dt.uint8), T.wc[:], [], [], "dw")
    dma("y", T.wp[:], T.ws[:], [], ["w"], "dw")
    dma("y", T.vt[:], T.v[:], [], ["vt"], "dv")

    cb, ct, sc, tb, lc, lr = T.cb, T.ct, T.sc, T.tb, T.lc, T.lr
    k16, k32 = cb[:, 0:16], cb[:, 0:32]
    q, val, fin = ct[:, 0:1], ct[:, 32:33], ct[:, 64:65]
    G32, GD, GF, GQ = lc[:, 0:2], lc[:, 2:6], lc[:, 6:8], lc[:, 8:44]
    KW, LS, L1, L2, HD, TL, LP = (lr[:, 0:32], lr[:, 32:64], lr[:, 64:96], lr[:, 96:132], lr[:, 132:136],
                                  lr[:, 136:140], lr[:, 140:172])
    iota(k32, [[0, 2], [1, 16]], 0, ["cb0"])
    iota(cb[:, 64:96], [[16, 2], [1, 8], [32, 2]], 0, ["cb2"])
    iota(cb[:, 128:136], [[-16, 8]], 0, ["pm"], 1)
    iota(cb[:, 96:128], [[1, 32]], 0, ["row"])
    iota(cb[:, 136:140], [[16, 2], [0, 2]], 0, ["dup"])
    if rank:
        fill(T.ones[:], 1.0, ["ones"])
        op("g", lambda: g.affine_select(T.ln[:, 0:PW], T.ones[:], [[-1, PW]], ALU.is_equal, 0.0, 3, 4), ["ones"], ["ln0"])
    iota(T.k16[:], [[0, 32], [1, 16]], 0, ["k16"])
    iota(T.jf[:], [[1, 32], [32, 16]], -H, ["jf"])
    iota(T.fl[:], [[0, SL]], -FAR, ["fl"])
    fill(T.zt[:], 0.0, ["z0"])
    ts(cb[:, 144:176], k32, 6.0, ALU.is_lt, ["cb0"], ["d0"], 2.0, ALU.mult)
    ts(cb[:, 176:208], k32, 0.0, ALU.is_equal, ["cb0"], ["d1"], -0.5, ALU.mult)
    fill(T.xs[:, C:C + 16], 0.0, ["xpad"])
    scan(cb[:, 32:64], cb[:, 144:176], cb[:, 176:208], 0.0, ALU.mult, ALU.add, ["d0", "d1"], ["cb1"])
    fill(T.pp[:, 0:4 * PW:PW], 0.0, ["pz"])
    tr(ct[:], cb[:, 0:96], ["cb0", "cb1", "cb2"], ["ct"])
    fill(T.et[:, 0 if last else 256:512], 0.0, ["epad"])
    for e in range(4):
        ts(T.zt[:, 48 + 5 * e:4 * ZW:64], cb[:, 128:136], q, ALU.is_equal, ["ct", "pm", "z0"], ["z%d" % (e + 1)], val, ALU.mult)
    act(tb[:, 0:32], k32, ACT.Identity, 0.0, 0.0, ["cb0"], ["tz0"])
    act(tb[:, 64:96], k32, ACT.Identity, 0.0, 0.0, ["cb0"], ["tz1"])
    for at, v in ((32, 1.0), (48, 2048.0), (96, 1.0), (112, 1.0 / 2048)):
        ts(tb[:, at:at + 16], k16, q, ALU.is_equal, ["ct"], ["te%d" % at], v, ALU.mult)
    quant(T.zq[:], T.zp[:], T.zt[:], ["z1", "z2", "z3", "z4"], ["zq"])
    ts(tb[:, 160:176], k16, q, ALU.is_lt, ["ct"], ["tl0"], 2048.0, ALU.add)
    ts(tb[:, 176:192], k16, q, ALU.is_lt, ["ct"], ["tl1"], 2048.0, ALU.mult)
    quant(T.uq[:], T.us[:], T.ut[:], ["ut"], ["u"])
    act(T.wa[:, 0:1], q, ACT.Identity, 4098.0, 65536.0, ["ct"], ["wa0"])
    act(T.wb[:, 0:1], q, ACT.Identity, 0.0, 2049.0, ["ct"], ["wb0"])
    act(sc[:, 2:3], q, ACT.Identity, 128.0, 160.0, ["ct"], ["sc2"])
    act(sc[:, 3:4], q, ACT.Identity, 32.0, 15.0, ["ct"], ["sc3"])
    act(sc[:, 4:5], q, ACT.Relu, 1024.0, -14336.0, ["ct"], ["sc4"])
    act(T.jw[:], cb[:, 96:128], ACT.Identity, 2048.0, sc[:, 2:3], ["row", "sc2"], ["jw"])
    act(tb[:, 272:288], tb[:, 31:47], ACT.Identity, 1024.0, 0.0, ["tz0", "te32"], ["tm2"])
    cp("s", tb[:, 128:160], tb[:, 96:128], ["te96", "te112"], ["te128"])
    cp("s", tb[:, 192:224], tb[:, 160:192], ["tl0", "tl1"], ["tl2"])
    steps, picks, starts = ["tz0", "tz1", "te32", "te48"], ["te96", "te112", "te128"], ["tl0", "tl1", "tl2"]

    def state(t, tile, n, rd):
        lo, hi = PART[n]
        quant(T["aq%d" % t][:, lo:hi], T["as%d" % t][:, lo:hi], tile[:, 4 * lo:4 * hi], rd, ["a%d_%d" % (t, n)])

    def product(name, n, t, lq_, ls_, rd):
        lo, hi = PART[n]
        mm(bank("p" + name, n, 0, hi - lo), lq_, ls_, T["aq%d" % t][:, lo:hi], T["as%d" % t][:, lo:hi],
           [rd, "a%d_%d" % (t, n)], ["@%s%d" % (name, n)])

    def plane(b):
        op("s", lambda: S.activation(T.pp[:, PW * b + 1:PW * b + C + 1], bank("pa", b, 0, C), ACT.Copy, scale=0.03125),
           ["@a%d" % b], ["p%d" % b])

    powers = [0] if rank else []
    for i in due(0, rank):
        if rank - 1 - i not in powers:
            powers.append(rank - 1 - i)
    lines, units = powers[1:], [(e, b) for e in powers for b in range(4)]

    def line(n):
        for e in lines[:n]:
            op("s", lambda: S.activation(T.ln[:, PW * e:PW * e + PW], T.ln[:, 0:PW], ACT.Copy, scale=0.5 ** e),
               ["ln0"], ["ln%d" % e])
        del lines[:n]

    def unit(n):
        for e, b in units[:n]:
            o, z = 512 * e + 128 * b, PW * e + 3 - b
            quant(T.iq[:, o:o + 128], T.ip[:, o:o + 128], T.ln[:, z:z + 512], ["ln%d" % e], ["i%d_%d" % (e, b)])
        del units[:n]

    def gap(n):
        if rank >= MANY:
            unit(n)

    def fields(at, half):
        x, y, tok = T.x4[:, 2 * half:2 * half + 2], 4 * half, "xy%d" % half
        return (lambda: cp("v", x, T.cum[:, at:at + 2], ["cumA", "cumB"], [tok]),
                lambda: ts(T.y8[:, y:y + 4:2], x, 2047, ALU.bitwise_and, [tok], [tok + "a"]),
                lambda: ts(T.y8[:, y + 1:y + 4:2], x, 11, ALU.logical_shift_right, [tok], [tok + "b"]),
                lambda: cp("v", TL if half else HD, T.y8[:, y:y + 4], [tok + "a", tok + "b"], ["TL" if half else "HD"]))

    for n in range(3):
        state(0, T.xt, n, ["xt%d" % (n // 2)])

    for t in range(R):
        aq, ap = T["aq%d" % t], T["as%d" % t]
        lq, lp = T["lq%d" % t], T["lp%d" % t]

        def layer(b):
            mm(bank("pa", b, 0, C), T.wq[:, 128 * b:128 * b + 128], T.wp[:, 128 * b:128 * b + 128], aq[:], ap[:],
               ["w"] + ["a%d_%d" % (t, n) for n in range(3)], ["@a%d" % b])
        for n in range(3):
            product("b", n, t, T.uq[:], T.us[:], "u")
            lo, hi = PART[n]
            act(T.xs[:, lo:hi], bank("pb", n, 0, hi - lo), ACT.Sign, 1.0, TINY, ["@b%d" % n], ["xs%d" % n])
        if t:
            layer(0)
            plane(0)
            quant(T.vq[:], T.vs[:], T.vt[:], ["vt"], ["v"])
        else:
            ts(T.r16[:], T.k16[:], 0.0, ALU.is_gt, ["k16"], ["r16"])
            ts(GQ, T.k16[:, 0:36], 0.0, ALU.mult, ["k16", "ct"], ["GQ"], q, ALU.add)
            line(1)
            gap(4)
        for h in range(2):
            quant(T["sq%d" % h][:], T["sp%d" % h][:], T.xs[:, 4 * h:4 * h + 4 * XW], ["xs0", "xs1", "xs2", "xpad"], ["sq%d" % h])
        for n, s in enumerate((0, 2, 1, 3)):
            o, z = s & 2, 12 - 4 * s
            mm(bank("pb", 3, 0, 128), T.zq[:, z:z + 128], T.zp[:, z:z + 128],
               T["sq%d" % (s & 1)][:, o:o + 128], T["sp%d" % (s & 1)][:, o:o + 128],
               ["zq", "sq%d" % (s & 1)], ["@b3"] if n in (0, 3) else [], n == 0, n == 3)
        for b in range(1 if t else 0, 4):
            layer(b)
        if t == 0:
            tt(tb[:, 224:240], tb[:, 272:288], tb[:, 48:64], ALU.subtract, ["tm2", "te48"], ["tm"])
            ts(G32, cb[:, 136:140:2], sc[:, 3:4], ALU.add, ["dup", "sc3"], ["G32"])
            gap(2)
        keys = bank("pb", 3, 0, 128, 4)
        ts(KW, keys, 31.5, ALU.add, ["@b3"], ["KW"])
        tt(T.tmp[:], keys, T.jw[:], ALU.add, ["@b3", "jw"], ["tmp"])
        op("s", lambda: S.activation(T.wl[:], tb[:, 160:224].indirect(KW), ACT.Copy, accum_out=T.acc[:, 0:1]),
           ["KW"] + starts, ["acc", "wl"])
        cp("v", T.wa[:, 1:C + 1], tb[:, 32:96].indirect(KW), ["KW"] + steps, ["wa"])
        cp("s", T.wb[:, 1:C + 1], tb[:, 0:64].indirect(KW), ["KW"] + steps, ["wb"])
        cp("s", T.wi[:, 0:16 * WS], tb[:, 96:160].indirect(lr[:, 0:WS]), ["KW"] + picks, ["wi"])
        ts(LS, T.tmp[:], 1.0 / 64, ALU.mult, ["tmp"], ["LS"])
        scan(T.cum[:, 0:2 * C + 2:2], T.wa[:, 0:C + 1], T.wa[:, 0:C + 1], T.acc[:, 0:1], ALU.add, ALU.max,
             ["wa", "wa0", "acc"], ["cumA"])
        cp("v", T.wi[:, 16 * WS:C], tb[:, 96:160].indirect(lr[:, WS:32]), ["KW"] + picks, ["wi2"])
        scan(T.cum[:, 1:2 * C + 2:2], T.wb[:, 0:C + 1], T.wb[:, 0:C + 1], T.cum[:, 2 * C:2 * C + 1], ALU.add, ALU.max,
             ["wb", "wb0", "cumA"], ["cumB"])
        for b in range(1 if t else 0, 4):
            plane(b)
        if t == 0:
            cp("s", T.dm[:], tb[:, 224:240].indirect(GQ), ["tm", "GQ"], ["dm"])
            line(N)
        nothing = (lambda: None,) * 4
        tails = nothing if last else fields(2 * C, 1)
        heads = fields(0, 0) if rank else nothing
        halves = ((0, H), (H, C))
        for n, (lo, hi) in enumerate(halves):
            tt(T.vv[:, lo:hi], T.cum[:, 0:2 * C + 2].indirect(lr[:, 32 + lo // 16:32 + hi // 16]), T.wi[:, lo:hi], ALU.mult,
               ["cumA", "cumB", "LS", "wi", "wi2"], ["vv%d" % n])
        for n, (lo, hi) in enumerate(halves):
            tr(T.vt2[:, lo:hi], T.vv[:, lo:hi], ["vv%d" % n], ["vt%d" % n])
        for n, (lo, hi) in enumerate(halves):
            scan(T.vs2[:, lo:hi], T.r16[:, lo:hi], T.vt2[:, lo:hi], 0.0, ALU.mult, ALU.add, ["vt%d" % n, "r16"], ["vs%d" % n])
        tails[0]()
        cp("v", T.y32[:], T.vs2[:].indirect(G32), ["vs0", "vs1", "G32"], ["y32"])
        tails[1]()
        tr(T.yt[:], T.y32[:], ["y32"], ["yt"])
        tails[2]()
        ts(T.za[:], T.yt[:], 2047, ALU.bitwise_and, ["yt"], ["za"])
        heads[0]()
        cp("v", LP, T.za[:], ["za"], ["LP"])
        tails[3]()
        gap(1)
        cp("v", T.fl[:].indirect(LP), T.jf[:], ["LP", "jf"], ["fl"])
        heads[1]()
        gap(1)
        act(T.mk[:], T.fl[:], ACT.Relu, 0.5 / FAR, 0.5, ["fl"], ["mk"])
        scan(T.dg[:], T.dm[:], T.fl[:], 0.0, ALU.add, ALU.max, ["dm", "fl"], ["dg"])
        heads[2]()
        ts(L2, T.dg[:, 15:SL:16], sc[:, 4:5], ALU.add, ["dg", "sc4"], ["L2"], float(H + 1 - 1024), ALU.add)
        heads[3]()
        gap(1)

        def srt(q_, b, lo=0, hi=SL // 16, part=""):
            cp(q_, T.ps[:, SL * b + 16 * lo:SL * b + 16 * hi],
               T.pp[:, PW * b:PW * b + C + 1].indirect(lr[:, 96 + lo:96 + hi]),
               ["L2", "pz", "p%d" % b], ["s%d%s" % (b, part)])

        def run(b):
            scan(T.hs[:, SL * b:SL * b + SL], T.mk[:], T.ps[:, SL * b:SL * b + SL], 0.0, ALU.mult, ALU.max,
                 ["mk", "s%d" % b, "s%dx" % b], ["h%d" % b])

        def tail(q_, b):
            cp(q_, T.et[:, b:256:4], T.hs[:, SL * b:SL * b + SL].indirect(TL), ["TL", "h%d" % b], ["e%d" % b])

        def back(q_, b, lo=0, hi=4):
            cp(q_, T.ht[:, C * lo + b:C * hi:4], T.hs[:, SL * b:SL * b + SL].indirect(lr[:, 64 + 8 * lo:64 + 8 * hi]),
               ["L1", "h%d" % b], ["ht%d_%d" % (b, h) for h in range(lo, hi)])

        def hand_on():
            to = [r for r in second if r != rank]
            for x in loads(t, rank):
                send(t, [(x[0], len(x), to[::-1] if t else to, near_mask(rank), "f")], x)

        if t:
            hand_on()
        srt("s", 1)
        srt("s", 2)
        srt("s", 3, 0, GS)
        srt("v", 0)
        srt("v", 3, GS, SL // 16, "x")
        if not last:
            for b in range(4):
                run(b)
            for b in range(3):
                tail("s", b)
        if t == 0:
            ts(GD, cb[:, 136:140], q, ALU.add, ["dup", "ct"], ["GD"])
        if not last:
            tail("v", 3)
        if t == 0:
            ts(GF, cb[:, 96:98], 8.0, ALU.mult, ["row", "ct"], ["GF"], fin, ALU.add)
        s0 = slot(t, rank, rank)
        quant(lq[:, K * s0:K * s0 + 128], lp[:, K * s0:K * s0 + 128], T.et[:],
              ["e0", "e1", "e2", "e3", "epad"], ["L%d_%d" % (t, s0), "M%d_%d" % (t, s0)])
        if not last:
            for call in plan(t, rank):
                send(t, [(rank, 1, to, m, kind) for to, m, kind in call], [rank])
        if t == 0:
            hand_on()
        cp("v", T.m64[:], T.za[:].indirect(GD), ["za", "GD"], ["m64"])
        unit(1)
        tr(T.mt[:], T.m64[:], ["m64"], ["mt"])
        if t == 0:
            fill(T.fl[:], float(-FAR), ["fl"])
            if rank:
                fill(T.cc[:, 256:512], 0.0, ["cpad"])
        cp("v", L1, T.mt[:].indirect(GF), ["mt", "GF"], ["L1"])
        unit(4 * N)

        def unpack(nm, e, cq_, cp_, rd):
            for b in range(4):
                o = 512 * e + 128 * b
                mm(bank("p" + nm, b, 0, 128), T.iq[:, o:o + 128], T.ip[:, o:o + 128], cq_, cp_,
                   ["i%d_%d" % (e, b)] + rd, ["@%s%d" % (nm, b)])

        if rank:
            seq = due(t, rank)
            cct = ["c%d" % b for b in range(4)]
            for n, i in enumerate(seq):
                lo = slot(t, rank, i)
                nm = "ba"[n % 2]
                unpack(nm, rank - 1 - i, lq[:, K * lo:K * lo + 128], lp[:, K * lo:K * lo + 128],
                       ["%s%d_%d" % (a, t, j) for a in "LM" for j in (lo, lo + 1)])
                for b in range(4):
                    src, out = bank("p" + nm, b, 0, K), T.cc[:, b:256:4]
                    if n == 0:
                        cp("s" if t else "v", out, src, ["@%s%d" % (nm, b)], [cct[b]])
                    else:
                        tt(out, src, out, ALU.max, ["@%s%d" % (nm, b), cct[b]], [cct[b]])
            quant(T.cq[:], T.cp[:], T.cc[:], cct + ["cpad"], ["cq"])
            nm = "ba"[len(seq) % 2]
            unpack(nm, 0, T.cq[:], T.cp[:], ["cq"])
            for b in range(4):
                cp("s" if b else "v", T.cs[:, K * b:K * b + K], bank("p" + nm, b, 0, K), ["@%s%d" % (nm, b)], ["cs%d" % b])

            def head(b):
                cp("v", T.ps[:, SL * b:SL * b + SL].indirect(HD), T.cs[:, K * b:K * b + K], ["HD", "cs%d" % b],
                   ["s%d" % b, "s%dx" % b])
            head(0)
            run(0)
            head(1)
            head(2)
            run(1)
            head(3)
            run(2)
            run(3)
            back("s", 0)
            back("s", 1)
        else:
            for b in range(2):
                back("sv"[b], b)
        back("s", 2, 0, 2)
        back("s", 2, 2, 4)
        back("s", 3, 3, 4)
        for n, (lo, hi) in enumerate(((0, 2), (2, 3), (3, 4))):
            if n < 2:
                back("v", 3, lo, hi)
            state(t + 1, T.ht, n, ["ht%d_%d" % (b, h) for b in range(4) for h in range(lo, hi)])

    aq, ap = T["aq%d" % R], T["as%d" % R]
    an = ["a%d_%d" % (R, n) for n in range(3)]
    for n in range(3):
        product("a", n, R, T.vq[:], T.vs[:], "v")
        cp("ssv"[n], T.ysb[:, PART[n][0]:PART[n][1]], bank("pa", n, 0, PART[n][1] - PART[n][0]), ["@a%d" % n], ["y%d" % n])
        if n == 0:
            dma("s", T.y[:, 0:H], T.ysb[:, 0:H], ["y0"], [], "dout2")
    dma("y", T.oc[:, 0:4 * H], aq[:, 0:H].bitcast(dt.uint8), an[:1], [], "dout")
    dma("y", T.oc[:, 4 * H:4 * C], aq[:, H:C].bitcast(dt.uint8), an[1:], [], "dout")
    for k in range(4):
        dma("y" if k < 3 else "s", T.osc[4 * k:4 * k + 4, :], ap[32 * k:32 * k + 4, :], an, [], "dout" if k < 3 else "dout2")
    dma("s", T.y[:, H:C], T.ysb[:, H:C], ["y1", "y2"], [], "dout2")
    for sem in ("cv", "cs", "ct", "cg", "dv", "dw", "dout", "dout2"):
        g.sync.wait_ge(T.sem[sem], count[sem])
    if "ls" in count:
        g.wait_ge(T.sem.ls, count["ls"])
